import numpy as np
import ml_dtypes


def mxq(x, axis, fmt="e4m3"):
    dtype, down = {"e4m3": (ml_dtypes.float8_e4m3fn, 7), "e5m2": (ml_dtypes.float8_e5m2, 14)}[fmt]
    v = np.moveaxis(np.asarray(x, np.float32).astype(ml_dtypes.bfloat16).astype(np.float64), axis, -1)
    blocks = v.reshape(v.shape[:-1] + (-1, 32))
    amax = np.abs(blocks).max(-1, keepdims=True)
    byte = np.maximum(np.where(amax > 0, np.frexp(amax)[1] - 1 + 127, 0) - down, 1)
    scale = np.exp2(byte - 127.0)
    codes = (blocks / scale).astype(np.float32).astype(dtype).astype(np.float64)
    return np.moveaxis((codes * scale).reshape(v.shape), -1, axis)


WIDE = False


def mx_kscale(k):
    if not WIDE:
        return np.ones(k)
    levels = np.array([10, -10, 5, -5, 0])
    if k % 512:
        return np.exp2(np.random.permutation(np.resize(levels, k // 32))).repeat(32)
    a = np.empty((k // 512, 16))
    for p in range(k // 512):
        a[p, :8] = np.random.permutation(np.resize(levels, 8))
        for g in range(8):
            far = levels[np.abs(levels - a[p, g]) >= 10]
            a[p, g + 8] = far[np.random.randint(len(far))]
    return np.exp2(a.ravel()).repeat(32)


def f64(x):
    return np.asarray(x).astype(np.float64)


def striped(idx):
    return np.tile(idx.reshape(-1, 16).T, (8, 1)).astype(np.uint16)


def unstriped(offs):
    return offs[:16].T.reshape(-1).astype(np.int64)


E2M1 = np.array([0.0, 0.5, 1.0, 1.5, 2.0, 3.0, 4.0, 6.0, -0.0, -0.5, -1.0, -1.5, -2.0, -3.0, -4.0, -6.0])


def pack_fp4(w):
    k, n = w.shape
    w = f64(np.asarray(w, np.float32).astype(ml_dtypes.bfloat16)).reshape(k // 32, 32, n)
    amax = np.abs(w).max(1)
    mant, ex = np.frexp(amax / 6.0)
    byte = np.clip(np.where(amax > 0, np.where(mant > 0.5, ex, ex - 1) + 127, 1), 1, 254)
    scaled = (w * np.exp2(127.0 - byte)[:, None, :]).reshape(k, n).astype(np.float32)
    c = np.ascontiguousarray(scaled.reshape(k // 512, 128, 4, n).transpose(0, 1, 3, 2)).astype(ml_dtypes.float4_e2m1fn).view(np.uint8) & 0xF
    words = (c[..., 0::2] | (c[..., 1::2] << 4)).reshape(k // 512, 128, 2 * n)
    return np.ascontiguousarray(words), np.ascontiguousarray(byte.astype(np.uint8).reshape(k // 512, 16, n))


def unpack_fp4(words, scales):
    g, _, n = scales.shape
    words = np.ascontiguousarray(words).reshape(g, 128, n, 2)
    nib = np.empty((g, 128, n, 4), np.uint8)
    nib[..., 0::2] = words & 0xF
    nib[..., 1::2] = words >> 4
    vals = E2M1[nib] * np.repeat(np.exp2(scales.astype(np.float64) - 127.0), 8, axis=1)[..., None]
    return vals.transpose(0, 1, 3, 2).reshape(g * 512, n)


K, T, S, D, V, H, N = 512, 1024, 512, 2, 256, 512, 256
P = 2 ** 7


def setup_inputs():
    n = np.random.standard_normal
    s = mx_kscale(K)[:, None]
    u = mx_kscale(H)
    packed_w2 = pack_fp4(n((H, N)) / np.sqrt(H) / u[:, None])
    return {
        "xT": (n((K, T)) * s).astype(np.float32),
        "w1": (n((K, H)) / np.sqrt(K) / s * u).astype(np.float32),
        "w2_words": packed_w2[0],
        "w2_scales": packed_w2[1],
        "gate": (np.tile(np.random.uniform(0.2, 1.0, (D, 1, V)) / np.sqrt(D), (1, P, 1))).astype(np.float32),
        "offs": striped(np.random.permutation(T)[:S]),
        "cen": striped(np.random.permutation(S)[:V]),
        "pos1": striped(np.random.permutation(S)[:V]),
        "pos2": striped(np.random.permutation(S)[:V]),
    }


def reference(xT, w1, w2_words, w2_scales, gate, offs, cen, pos1, pos2):
    xq = mxq(f64(xT)[:, unstriped(offs)], 0, "e4m3")
    h = mxq(f64(w1), 0, "e4m3").T @ xq
    z = h[:, unstriped(cen)] - (h[:, unstriped(pos1)] * f64(gate)[0, :1] + h[:, unstriped(pos2)] * f64(gate)[1, :1])
    return unpack_fp4(w2_words, w2_scales).T @ mxq(z, 0, "e4m3")

@@ -1,0 +1,174 @@
+from contextlib import ExitStack
+
+import concourse.mybir as mybir
+
+K, T, S, V, H, N = 512, 1024, 512, 256, 512, 256
+FLOPS = 2 * K * H * S + 2 * H * N * V
+
+F32 = mybir.dt.float32
+BF16 = mybir.dt.bfloat16
+I32 = mybir.dt.int32
+U32 = mybir.dt.uint32
+U16 = mybir.dt.uint16
+U8 = mybir.dt.uint8
+FP8X4 = mybir.dt.float8_e4m3fn_x4
+FP4X4 = mybir.dt.float4_e2m1fn_x4
+MULT = mybir.AluOpType.mult
+SUB = mybir.AluOpType.subtract
+
+P = 128
+PACK = 4
+LIST = 16
+HALF_T = T // 2
+HALF_S = S // 2
+HALF_H = H // 2
+HALF_V = V // 2
+X_VECTOR_NODES = {(0, 0): 512, (0, 1): 320, (1, 0): 0, (1, 1): 384}
+W_SCALAR_ROWS = {0: 64, 1: 32}
+
+
+def tile_picked_lapl_none_e_kernel(
+    tc, xT, w1, w2_words, w2_scales, gate, offs, cen, pos1, pos2, out
+):
+    nc = tc.nc
+    with ExitStack() as ctx:
+        keep = ctx.enter_context(tc.tile_pool(name="keep", bufs=1))
+        psum = ctx.enter_context(tc.psum_pool(name="psum", bufs=1))
+
+        offs_sb = keep.tile([P, S // LIST], U16, name="offs_sb")
+        cen_sb = keep.tile([P, V // LIST], U16, name="cen_sb")
+        pos1_sb = keep.tile([P, V // LIST], U16, name="pos1_sb")
+        pos2_sb = keep.tile([P, V // LIST], U16, name="pos2_sb")
+        gate_sb = keep.tile([P, 2, V], F32, name="gate_sb")
+        w2_codes = keep.tile([P, 2 * N], U8, name="w2_codes", align_bytes=64)
+        w2_plane = keep.tile([P, N], U8, name="w2_plane", align_bytes=64)
+        nc.gpsimd.memset(w2_plane[:], 0)
+
+        x_rows = xT.rearrange("(p j) t -> p j t", j=PACK)
+        w_rows = w1.rearrange("(p j) c -> p j c", j=PACK)
+        x_raw = {}
+        for u in range(2):
+            for c in range(2):
+                x_raw[u, c] = keep.tile([P, 2, HALF_T], F32, name=f"x_raw{u}{c}")
+                nc.sync.dma_start(x_raw[u, c][:], x_rows[:, 2 * u : 2 * u + 2, c * HALF_T : (c + 1) * HALF_T])
+                if (u, c) == (0, 0):
+                    nc.sync.dma_start(offs_sb[:], offs)
+        w_raw = []
+        for c in range(2):
+            w_raw.append(keep.tile([P, PACK, HALF_H], F32, name=f"w_raw{c}"))
+            nc.sync.dma_start(w_raw[c][:], w_rows[:, :, c * HALF_H : (c + 1) * HALF_H])
+        nc.sync.dma_start(pos1_sb[:], pos1)
+        nc.sync.dma_start(gate_sb[:], gate.rearrange("d p v -> p d v"))
+        nc.sync.dma_start(pos2_sb[:], pos2)
+        nc.sync.dma_start(cen_sb[:], cen)
+        nc.sync.dma_start(w2_codes[:].bitcast(I32), w2_words[0].bitcast(I32))
+        for q in range(4):
+            nc.sync.dma_start(
+                w2_plane[32 * q : 32 * q + 4, :].bitcast(I32), w2_scales[0, 4 * q : 4 * q + 4, :].bitcast(I32)
+            )
+
+        x_pick = [keep.tile([P, HALF_S * PACK], BF16, name=f"x_pick{c}", align_bytes=64) for c in range(2)]
+        for u in range(2):
+            pairs = keep.tile([P, T * 2], BF16, name=f"x_pairs{u}")
+            for c in range(2):
+                cut = X_VECTOR_NODES[u, c]
+                for lo, hi, copy in ((0, cut, nc.vector.tensor_copy), (cut, HALF_T, nc.scalar.copy)):
+                    if hi > lo:
+                        dst = pairs[:, 2 * (c * HALF_T + lo) : 2 * (c * HALF_T + hi)]
+                        copy(
+                            dst.rearrange("p (a i e) -> p a e i", i=4, e=2),
+                            x_raw[u, c][:, :, lo:hi].rearrange("p e (a i) -> p a e i", i=4),
+                        )
+            for c in range(2):
+                cols = slice(c * HALF_S // LIST, (c + 1) * HALF_S // LIST)
+                nc.vector.tensor_copy(
+                    x_pick[c][:].bitcast(U32).rearrange("p (s u) -> p s u", u=2)[:, :, u],
+                    pairs[:].bitcast(U32).indirect(offs_sb[:, cols]),
+                )
+        x_codes = keep.tile([P, S], U32, name="x_codes", align_bytes=64)
+        x_plane = keep.tile([P, S], U8, name="x_plane", align_bytes=64)
+        for c in range(2):
+            cols = slice(c * HALF_S, (c + 1) * HALF_S)
+            nc.vector.quantize_mx(out=x_codes[:, cols].bitcast(FP8X4), scales=x_plane[:, cols], in_=x_pick[c][:])
+
+        w_dealt = keep.tile([P, H * PACK], BF16, name="w_dealt", align_bytes=64)
+        w_view = w_dealt[:].rearrange("p (t m j) -> p m j t", t=PACK, j=PACK)
+        rows = HALF_H // PACK
+        for c in range(2):
+            cut = W_SCALAR_ROWS[c]
+            src = w_raw[c][:].rearrange("p j (m t) -> p m j t", t=PACK)
+            for lo, hi, copy in ((0, cut, nc.scalar.copy), (cut, rows, nc.vector.tensor_copy)):
+                if hi > lo:
+                    copy(w_view[:, c * rows + lo : c * rows + hi], src[:, lo:hi])
+        w_codes = keep.tile([P, H], U32, name="w_codes", align_bytes=64)
+        w_plane = keep.tile([P, H], U8, name="w_plane", align_bytes=64)
+        for lo, hi in ((0, P), (P, 2 * P), (2 * P, H)):
+            nc.vector.quantize_mx(
+                out=w_codes[:, lo:hi].bitcast(FP8X4), scales=w_plane[:, lo:hi], in_=w_dealt[:, PACK * lo : PACK * hi]
+            )
+
+        h_sb = []
+        for t in range(PACK):
+            h_sb.append(keep.tile([P, S], F32, name=f"h_sb{t}"))
+            m_cols = slice(t * P, (t + 1) * P)
+            if t == 0:
+                parts = ((0, HALF_S, nc.scalar.copy), (HALF_S, S, nc.vector.tensor_copy))
+            else:
+                parts = ((0, S, nc.scalar.copy),)
+            for lo, hi, copy in parts:
+                acc = psum.tile([P, hi - lo], F32, name=f"h_ps{t}_{lo}")
+                nc.tensor.matmul_mx(
+                    out=acc[:],
+                    lhsT=w_codes[:, m_cols].bitcast(FP8X4),
+                    lhsT_scale=w_plane[:, m_cols],
+                    rhs=x_codes[:, lo:hi].bitcast(FP8X4),
+                    rhs_scale=x_plane[:, lo:hi],
+                    start=True,
+                    stop=True,
+                )
+                copy(h_sb[t][:, lo:hi], acc[:])
+
+        first = keep.tile([P, PACK, V], F32, name="first")
+        second = keep.tile([P, PACK, V], F32, name="second")
+        rest = keep.tile([P, PACK, V], F32, name="rest")
+        for t in range(PACK):
+            nc.vector.tensor_tensor(first[:, t, :], h_sb[t][:].indirect(pos1_sb[:]), gate_sb[:, 0, :], MULT)
+            nc.vector.tensor_tensor(second[:, t, :], h_sb[t][:].indirect(pos2_sb[:]), gate_sb[:, 1, :], MULT)
+            if t < PACK - 1:
+                nc.vector.tensor_tensor(rest[:, t, :], h_sb[t][:].indirect(cen_sb[:]), first[:, t, :], SUB)
+            else:
+                for c in range(2):
+                    cols = slice(c * HALF_V, (c + 1) * HALF_V)
+                    lst = cen_sb[:, c * HALF_V // LIST : (c + 1) * HALF_V // LIST]
+                    nc.vector.tensor_tensor(rest[:, t, cols], h_sb[t][:].indirect(lst), first[:, t, cols], SUB)
+
+        z = []
+        for c in range(2):
+            cols = slice(c * HALF_V, (c + 1) * HALF_V)
+            z.append(keep.tile([P, HALF_V * PACK], BF16, name=f"z{c}", align_bytes=64))
+            nc.vector.tensor_tensor(
+                z[c][:].rearrange("p (a i t) -> p a t i", i=4, t=PACK),
+                rest[:, :, cols].rearrange("p t (a i) -> p a t i", i=4),
+                second[:, :, cols].rearrange("p t (a i) -> p a t i", i=4),
+                SUB,
+            )
+        out_ps = [psum.tile([P, V], F32, name=f"out_ps{m}") for m in range(2)]
+        for c in range(2):
+            cols = slice(c * HALF_V, (c + 1) * HALF_V)
+            z_codes = keep.tile([P, HALF_V], U32, name=f"z_codes{c}", align_bytes=64)
+            z_plane = keep.tile([P, HALF_V], U8, name=f"z_plane{c}", align_bytes=64)
+            nc.vector.quantize_mx(out=z_codes[:].bitcast(FP8X4), scales=z_plane[:], in_=z[c][:])
+            for m in range(2):
+                nc.tensor.matmul_mx(
+                    out=out_ps[m][:, cols],
+                    lhsT=w2_codes[:, 2 * m * P : 2 * (m + 1) * P].bitcast(FP4X4),
+                    lhsT_scale=w2_plane[:, m * P : (m + 1) * P],
+                    rhs=z_codes[:].bitcast(FP8X4),
+                    rhs_scale=z_plane[:],
+                    start=True,
+                    stop=True,
+                )
+        for m, (copy, queue) in enumerate(((nc.scalar.copy, nc.scalar), (nc.vector.tensor_copy, nc.sync))):
+            res = keep.tile([P, V], F32, name=f"res{m}")
+            copy(res[:], out_ps[m][:])
+            queue.dma_start(out[m * P : (m + 1) * P, :], res[:])

@@ -1,6 +1,7 @@
 from contextlib import ExitStack
 
 import concourse.mybir as mybir
+from concourse.masks import make_identity
 
 K, T, S, V, H, N = 512, 1024, 512, 256, 512, 256
 FLOPS = 2 * K * H * S + 2 * H * N * V
@@ -14,17 +15,17 @@ U8 = mybir.dt.uint8
 FP8X4 = mybir.dt.float8_e4m3fn_x4
 FP4X4 = mybir.dt.float4_e2m1fn_x4
 MULT = mybir.AluOpType.mult
+ADD = mybir.AluOpType.add
 SUB = mybir.AluOpType.subtract
 
 P = 128
 PACK = 4
 LIST = 16
-HALF_T = T // 2
-HALF_S = S // 2
 HALF_H = H // 2
 HALF_V = V // 2
-X_VECTOR_NODES = {(0, 0): 512, (0, 1): 320, (1, 0): 0, (1, 1): 384}
-W_SCALAR_ROWS = {0: 64, 1: 32}
+HALF_P = P // 2
+X_LOADS = (((0, 640, 640), (640, 1024, 896)), ((0, 512, 0), (512, 768, 768), (768, 1024, 928)))
+PICK_PARTS = ((0, 256), (256, 384), (384, 512))
 
 
 def tile_picked_lapl_none_e_kernel(
@@ -39,26 +40,28 @@ def tile_picked_lapl_none_e_kernel(
         cen_sb = keep.tile([P, V // LIST], U16, name="cen_sb")
         pos1_sb = keep.tile([P, V // LIST], U16, name="pos1_sb")
         pos2_sb = keep.tile([P, V // LIST], U16, name="pos2_sb")
-        gate_sb = keep.tile([P, 2, V], F32, name="gate_sb")
+        gate_sb = [keep.tile([P, V], F32, name=f"gate_sb{d}") for d in range(2)]
         w2_codes = keep.tile([P, 2 * N], U8, name="w2_codes", align_bytes=64)
         w2_plane = keep.tile([P, N], U8, name="w2_plane", align_bytes=64)
         nc.gpsimd.memset(w2_plane[:], 0)
+        ident = keep.tile([P, P], F32, name="ident")
+        make_identity(nc, ident[:])
 
         x_rows = xT.rearrange("(p j) t -> p j t", j=PACK)
         w_rows = w1.rearrange("(p j) c -> p j c", j=PACK)
         x_raw = {}
         for u in range(2):
-            for c in range(2):
-                x_raw[u, c] = keep.tile([P, 2, HALF_T], F32, name=f"x_raw{u}{c}")
-                nc.sync.dma_start(x_raw[u, c][:], x_rows[:, 2 * u : 2 * u + 2, c * HALF_T : (c + 1) * HALF_T])
-                if (u, c) == (0, 0):
+            for lo, hi, cut in X_LOADS[u]:
+                x_raw[u, lo] = keep.tile([P, 2, hi - lo], F32, name=f"x_raw{u}_{lo}")
+                nc.sync.dma_start(x_raw[u, lo][:], x_rows[:, 2 * u : 2 * u + 2, lo:hi])
+                if (u, lo) == (0, 0):
                     nc.sync.dma_start(offs_sb[:], offs)
-        w_raw = []
-        for c in range(2):
-            w_raw.append(keep.tile([P, PACK, HALF_H], F32, name=f"w_raw{c}"))
-            nc.sync.dma_start(w_raw[c][:], w_rows[:, :, c * HALF_H : (c + 1) * HALF_H])
+        w_raw = [keep.tile([P, PACK, HALF_H], F32, name=f"w_raw{c}") for c in range(2)]
+        nc.sync.dma_start(w_raw[0][:], w_rows[:, :, :HALF_H])
+        nc.sync.dma_start(gate_sb[1][:], gate[1])
+        nc.sync.dma_start(w_raw[1][:], w_rows[:, :, HALF_H:])
         nc.sync.dma_start(pos1_sb[:], pos1)
-        nc.sync.dma_start(gate_sb[:], gate.rearrange("d p v -> p d v"))
+        nc.sync.dma_start(gate_sb[0][:], gate[0])
         nc.sync.dma_start(pos2_sb[:], pos2)
         nc.sync.dma_start(cen_sb[:], cen)
         nc.sync.dma_start(w2_codes[:].bitcast(I32), w2_words[0].bitcast(I32))
@@ -67,108 +70,155 @@ def tile_picked_lapl_none_e_kernel(
                 w2_plane[32 * q : 32 * q + 4, :].bitcast(I32), w2_scales[0, 4 * q : 4 * q + 4, :].bitcast(I32)
             )
 
-        x_pick = [keep.tile([P, HALF_S * PACK], BF16, name=f"x_pick{c}", align_bytes=64) for c in range(2)]
+        x_pick = keep.tile([P, S * PACK], BF16, name="x_pick", align_bytes=64)
         for u in range(2):
             pairs = keep.tile([P, T * 2], BF16, name=f"x_pairs{u}")
-            for c in range(2):
-                cut = X_VECTOR_NODES[u, c]
-                for lo, hi, copy in ((0, cut, nc.vector.tensor_copy), (cut, HALF_T, nc.scalar.copy)):
+            for base, end, cut in X_LOADS[u]:
+                for lo, hi, copy in ((base, cut, nc.vector.tensor_copy), (cut, end, nc.scalar.copy)):
                     if hi > lo:
-                        dst = pairs[:, 2 * (c * HALF_T + lo) : 2 * (c * HALF_T + hi)]
                         copy(
-                            dst.rearrange("p (a i e) -> p a e i", i=4, e=2),
-                            x_raw[u, c][:, :, lo:hi].rearrange("p e (a i) -> p a e i", i=4),
+                            pairs[:, 2 * lo : 2 * hi].rearrange("p (a i e) -> p a e i", i=4, e=2),
+                            x_raw[u, base][:, :, lo - base : hi - base].rearrange("p e (a i) -> p a e i", i=4),
                         )
-            for c in range(2):
-                cols = slice(c * HALF_S // LIST, (c + 1) * HALF_S // LIST)
-                nc.vector.tensor_copy(
-                    x_pick[c][:].bitcast(U32).rearrange("p (s u) -> p s u", u=2)[:, :, u],
-                    pairs[:].bitcast(U32).indirect(offs_sb[:, cols]),
-                )
-        x_codes = keep.tile([P, S], U32, name="x_codes", align_bytes=64)
-        x_plane = keep.tile([P, S], U8, name="x_plane", align_bytes=64)
-        for c in range(2):
-            cols = slice(c * HALF_S, (c + 1) * HALF_S)
-            nc.vector.quantize_mx(out=x_codes[:, cols].bitcast(FP8X4), scales=x_plane[:, cols], in_=x_pick[c][:])
-
-        w_dealt = keep.tile([P, H * PACK], BF16, name="w_dealt", align_bytes=64)
-        w_view = w_dealt[:].rearrange("p (t m j) -> p m j t", t=PACK, j=PACK)
-        rows = HALF_H // PACK
-        for c in range(2):
-            cut = W_SCALAR_ROWS[c]
-            src = w_raw[c][:].rearrange("p j (m t) -> p m j t", t=PACK)
-            for lo, hi, copy in ((0, cut, nc.scalar.copy), (cut, rows, nc.vector.tensor_copy)):
-                if hi > lo:
-                    copy(w_view[:, c * rows + lo : c * rows + hi], src[:, lo:hi])
-        w_codes = keep.tile([P, H], U32, name="w_codes", align_bytes=64)
-        w_plane = keep.tile([P, H], U8, name="w_plane", align_bytes=64)
-        for lo, hi in ((0, P), (P, 2 * P), (2 * P, H)):
-            nc.vector.quantize_mx(
-                out=w_codes[:, lo:hi].bitcast(FP8X4), scales=w_plane[:, lo:hi], in_=w_dealt[:, PACK * lo : PACK * hi]
+            nc.vector.tensor_copy(
+                x_pick[:].bitcast(U32).rearrange("p (s u) -> p s u", u=2)[:, :, u],
+                pairs[:].bitcast(U32).indirect(offs_sb[:]),
             )
 
-        h_sb = []
-        for t in range(PACK):
-            h_sb.append(keep.tile([P, S], F32, name=f"h_sb{t}"))
-            m_cols = slice(t * P, (t + 1) * P)
-            if t == 0:
-                parts = ((0, HALF_S, nc.scalar.copy), (HALF_S, S, nc.vector.tensor_copy))
-            else:
-                parts = ((0, S, nc.scalar.copy),)
-            for lo, hi, copy in parts:
-                acc = psum.tile([P, hi - lo], F32, name=f"h_ps{t}_{lo}")
-                nc.tensor.matmul_mx(
-                    out=acc[:],
-                    lhsT=w_codes[:, m_cols].bitcast(FP8X4),
-                    lhsT_scale=w_plane[:, m_cols],
-                    rhs=x_codes[:, lo:hi].bitcast(FP8X4),
-                    rhs_scale=x_plane[:, lo:hi],
-                    start=True,
-                    stop=True,
-                )
-                copy(h_sb[t][:, lo:hi], acc[:])
+        def deal(dst, c, first):
+            nc.scalar.copy(dst, w_raw[c][:].rearrange("p j (m t) -> p m j t", t=PACK)[:, :, :, first : first + 2])
+
+        def quantise(name, src, width):
+            codes = keep.tile([P, width], U32, name=f"{name}_codes", align_bytes=64)
+            plane = keep.tile([P, width], U8, name=f"{name}_plane", align_bytes=64)
+            nc.vector.quantize_mx(out=codes[:].bitcast(FP8X4), scales=plane[:], in_=src)
+            return codes, plane
+
+        def low_weights(c):
+            dealt = keep.tile([P, P * PACK], BF16, name=f"w_low{c}", tag=f"w_low{c}", align_bytes=64)
+            deal(dealt[:].rearrange("p (e m j) -> p m j e", e=2, j=PACK), c, 0)
+            return quantise(f"w_low{c}", dealt[:], P)
+
+        codes0, plane0 = low_weights(0)
+        x_codes = keep.tile([P, S], U32, name="x_codes", tag="w_low0", align_bytes=64)
+        x_plane = keep.tile([P, S], U8, name="x_plane", align_bytes=64)
+
+        def project(acc, codes, plane, lo, hi):
+            nc.tensor.matmul_mx(
+                out=acc,
+                lhsT=codes.bitcast(FP8X4),
+                lhsT_scale=plane,
+                rhs=x_codes[:, lo:hi].bitcast(FP8X4),
+                rhs_scale=x_plane[:, lo:hi],
+                start=True,
+                stop=True,
+            )
+
+        h_sb = [keep.tile([P, S], F32, name=f"h_sb{n}") for n in range(PACK)]
+        for lo, hi in PICK_PARTS:
+            nc.vector.quantize_mx(
+                out=x_codes[:, lo:hi].bitcast(FP8X4), scales=x_plane[:, lo:hi], in_=x_pick[:, PACK * lo : PACK * hi]
+            )
+        for tag, (lo, hi) in zip(("bank_a", "bank_b", "bank_c"), PICK_PARTS):
+            bank = psum.tile([P, hi - lo], F32, name=f"h_part{lo}", tag=tag)
+            project(bank[:], codes0[:], plane0[:], lo, hi)
+            nc.vector.tensor_copy(h_sb[0][:, lo:hi], bank[:])
+
+        minus_gate = keep.tile([P, V], F32, name="minus_gate")
+        nc.scalar.mul(minus_gate[:], gate_sb[1][:], -1.0)
+
+        codes1, plane1 = low_weights(1)
+        bank_c = psum.tile([P, S], F32, name="bank_low1")
+        project(bank_c[:], codes1[:], plane1[:], 0, S)
+        nc.scalar.copy(h_sb[1][:], bank_c[:])
+
+        w_high = keep.tile([P, 2 * P * PACK], BF16, name="w_high", align_bytes=64)
+        high_view = w_high[:].rearrange("p (e m j) -> p m j e", e=2, j=PACK)
+        for c in range(2):
+            deal(high_view[:, c * HALF_P : (c + 1) * HALF_P], c, 2)
+        codes_high, plane_high = quantise("w_high", w_high[:], 2 * P)
+        for e in range(2):
+            bank = psum.tile([P, S], F32, name=f"bank_high{e}")
+            project(bank[:], codes_high[:, e * P : (e + 1) * P], plane_high[:, e * P : (e + 1) * P], 0, S)
+            nc.scalar.copy(h_sb[2 + e][:], bank[:])
 
         first = keep.tile([P, PACK, V], F32, name="first")
         second = keep.tile([P, PACK, V], F32, name="second")
         rest = keep.tile([P, PACK, V], F32, name="rest")
-        for t in range(PACK):
-            nc.vector.tensor_tensor(first[:, t, :], h_sb[t][:].indirect(pos1_sb[:]), gate_sb[:, 0, :], MULT)
-            nc.vector.tensor_tensor(second[:, t, :], h_sb[t][:].indirect(pos2_sb[:]), gate_sb[:, 1, :], MULT)
-            if t < PACK - 1:
-                nc.vector.tensor_tensor(rest[:, t, :], h_sb[t][:].indirect(cen_sb[:]), first[:, t, :], SUB)
-            else:
+
+        def fetch(dst, n, places, other, op, c=None):
+            cols = slice(0, V) if c is None else slice(c * HALF_V, (c + 1) * HALF_V)
+            window = h_sb[n][:].indirect(places[:, cols.start // LIST : cols.stop // LIST])
+            nc.vector.tensor_tensor(dst[:, n, cols], window, other[:, cols], op)
+
+        z = [keep.tile([P, HALF_V * PACK], BF16, name=f"z{c}", align_bytes=64) for c in range(2)]
+        turned = psum.tile([P, 2, 2, P], F32, name="turned")
+        back = psum.tile([P, 2, HALF_V], F32, name="back")
+
+        for n in range(PACK - 1):
+            fetch(first, n, pos1_sb, gate_sb[0][:], MULT)
+            fetch(second, n, pos2_sb, minus_gate[:], MULT)
+            fetch(rest, n, cen_sb, first[:, n, :], SUB)
+            if n < 2:
                 for c in range(2):
                     cols = slice(c * HALF_V, (c + 1) * HALF_V)
-                    lst = cen_sb[:, c * HALF_V // LIST : (c + 1) * HALF_V // LIST]
-                    nc.vector.tensor_tensor(rest[:, t, cols], h_sb[t][:].indirect(lst), first[:, t, cols], SUB)
+                    for term, begin in ((second, True), (rest, False)):
+                        nc.tensor.matmul(
+                            turned[:, c, n, :], term[:, n, cols], ident[:], start=begin, stop=not begin, is_transpose=True
+                        )
+            if n == 1:
+                for c in range(2):
+                    rows = keep.tile([P, 2 * P], BF16, name=f"z_rows{c}")
+                    nc.scalar.copy(
+                        rows[:].rearrange("v (g m e) -> v g m e", g=2, e=2),
+                        turned[:, c].rearrange("v g (e m) -> v g m e", e=2),
+                    )
+                    nc.tensor.transpose(back[:, c, :], rows[:].bitcast(F32), ident[:])
+                    nc.scalar.copy(z[c][:].bitcast(F32).rearrange("p (v u) -> p v u", u=2)[:, :, 0], back[:, c, :])
 
-        z = []
-        for c in range(2):
+        def finish(c):
             cols = slice(c * HALF_V, (c + 1) * HALF_V)
-            z.append(keep.tile([P, HALF_V * PACK], BF16, name=f"z{c}", align_bytes=64))
             nc.vector.tensor_tensor(
-                z[c][:].rearrange("p (a i t) -> p a t i", i=4, t=PACK),
-                rest[:, :, cols].rearrange("p t (a i) -> p a t i", i=4),
-                second[:, :, cols].rearrange("p t (a i) -> p a t i", i=4),
-                SUB,
+                z[c][:].rearrange("p (a i t) -> p a t i", i=4, t=PACK)[:, :, 2:, :],
+                rest[:, 2:, cols].rearrange("p t (a i) -> p a t i", i=4),
+                second[:, 2:, cols].rearrange("p t (a i) -> p a t i", i=4),
+                ADD,
             )
-        out_ps = [psum.tile([P, V], F32, name=f"out_ps{m}") for m in range(2)]
-        for c in range(2):
-            cols = slice(c * HALF_V, (c + 1) * HALF_V)
-            z_codes = keep.tile([P, HALF_V], U32, name=f"z_codes{c}", align_bytes=64)
-            z_plane = keep.tile([P, HALF_V], U8, name=f"z_plane{c}", align_bytes=64)
-            nc.vector.quantize_mx(out=z_codes[:].bitcast(FP8X4), scales=z_plane[:], in_=z[c][:])
-            for m in range(2):
-                nc.tensor.matmul_mx(
-                    out=out_ps[m][:, cols],
-                    lhsT=w2_codes[:, 2 * m * P : 2 * (m + 1) * P].bitcast(FP4X4),
-                    lhsT_scale=w2_plane[:, m * P : (m + 1) * P],
-                    rhs=z_codes[:].bitcast(FP8X4),
-                    rhs_scale=z_plane[:],
-                    start=True,
-                    stop=True,
-                )
-        for m, (copy, queue) in enumerate(((nc.scalar.copy, nc.scalar), (nc.vector.tensor_copy, nc.sync))):
-            res = keep.tile([P, V], F32, name=f"res{m}")
-            copy(res[:], out_ps[m][:])
-            queue.dma_start(out[m * P : (m + 1) * P, :], res[:])
+
+        def second_product(acc, m, codes, plane):
+            nc.tensor.matmul_mx(
+                out=acc,
+                lhsT=w2_codes[:, 2 * m * P : 2 * (m + 1) * P].bitcast(FP4X4),
+                lhsT_scale=w2_plane[:, m * P : (m + 1) * P],
+                rhs=codes[:].bitcast(FP8X4),
+                rhs_scale=plane[:],
+                start=True,
+                stop=True,
+            )
+
+        last = PACK - 1
+        fetch(first, last, pos1_sb, gate_sb[0][:], MULT)
+        fetch(second, last, pos2_sb, minus_gate[:], MULT, 0)
+        fetch(rest, last, cen_sb, first[:, last, :], SUB, 0)
+        fetch(second, last, pos2_sb, minus_gate[:], MULT, 1)
+        finish(0)
+        fetch(rest, last, cen_sb, first[:, last, :], SUB, 1)
+        z_codes0, z_plane0 = quantise("z0", z[0][:], HALF_V)
+        finish(1)
+        z_codes1, z_plane1 = quantise("z1", z[1][:], HALF_V)
+
+        out_rows = out.rearrange("(m p) v -> p m v", p=P)
+        early_ps = psum.tile([P, 2, HALF_V], F32, name="early_ps", tag="bank_a")
+        for m in range(2):
+            second_product(early_ps[:, m, :], m, z_codes0, z_plane0)
+        early = keep.tile([P, 2, HALF_V], F32, name="early")
+        nc.scalar.copy(early[:], early_ps[:])
+        nc.sync.dma_start(out_rows[:, :, :HALF_V], early[:])
+        for m, (tag, copy, queue) in enumerate(
+            (("bank_b", nc.scalar.copy, nc.scalar), ("bank_c", nc.vector.tensor_copy, nc.sync))
+        ):
+            late_ps = psum.tile([P, HALF_V], F32, name=f"late_ps{m}", tag=tag)
+            second_product(late_ps[:], m, z_codes1, z_plane1)
+            late = keep.tile([P, HALF_V], F32, name=f"late{m}")
+            copy(late[:], late_ps[:])
+            queue.dma_start(out_rows[:, m, HALF_V:], late[:])

@@ -23,8 +23,7 @@ PACK = 4
 LIST = 16
 HALF_H = H // 2
 HALF_V = V // 2
-HALF_P = P // 2
-X_LOADS = (((0, 640, 640), (640, 1024, 896)), ((0, 512, 0), (512, 768, 768), (768, 1024, 928)))
+X_LOADS = (((0, 640, 640), (640, 1024, 1024)), ((0, 512, 0), (512, 768, 768), (768, 1024, 928)))
 PICK_PARTS = ((0, 256), (256, 384), (384, 512))
 
 
@@ -56,10 +55,10 @@ def tile_picked_lapl_none_e_kernel(
                 nc.sync.dma_start(x_raw[u, lo][:], x_rows[:, 2 * u : 2 * u + 2, lo:hi])
                 if (u, lo) == (0, 0):
                     nc.sync.dma_start(offs_sb[:], offs)
-        w_raw = [keep.tile([P, PACK, HALF_H], F32, name=f"w_raw{c}") for c in range(2)]
-        nc.sync.dma_start(w_raw[0][:], w_rows[:, :, :HALF_H])
+        w_raw = keep.tile([P, 2, PACK, HALF_H], F32, name="w_raw")
+        nc.sync.dma_start(w_raw[:, 0], w_rows[:, :, :HALF_H])
         nc.sync.dma_start(gate_sb[1][:], gate[1])
-        nc.sync.dma_start(w_raw[1][:], w_rows[:, :, HALF_H:])
+        nc.sync.dma_start(w_raw[:, 1], w_rows[:, :, HALF_H:])
         nc.sync.dma_start(pos1_sb[:], pos1)
         nc.sync.dma_start(gate_sb[0][:], gate[0])
         nc.sync.dma_start(pos2_sb[:], pos2)
@@ -85,8 +84,7 @@ def tile_picked_lapl_none_e_kernel(
                 pairs[:].bitcast(U32).indirect(offs_sb[:]),
             )
 
-        def deal(dst, c, first):
-            nc.scalar.copy(dst, w_raw[c][:].rearrange("p j (m t) -> p m j t", t=PACK)[:, :, :, first : first + 2])
+        w_cols = w_raw[:].rearrange("p c j (m t) -> p c m j t", t=PACK)
 
         def quantise(name, src, width):
             codes = keep.tile([P, width], U32, name=f"{name}_codes", align_bytes=64)
@@ -96,7 +94,7 @@ def tile_picked_lapl_none_e_kernel(
 
         def low_weights(c):
             dealt = keep.tile([P, P * PACK], BF16, name=f"w_low{c}", tag=f"w_low{c}", align_bytes=64)
-            deal(dealt[:].rearrange("p (e m j) -> p m j e", e=2, j=PACK), c, 0)
+            nc.scalar.copy(dealt[:].rearrange("p (e m j) -> p m j e", e=2, j=PACK), w_cols[:, c, :, :, :2])
             return quantise(f"w_low{c}", dealt[:], P)
 
         codes0, plane0 = low_weights(0)
@@ -133,9 +131,7 @@ def tile_picked_lapl_none_e_kernel(
         nc.scalar.copy(h_sb[1][:], bank_c[:])
 
         w_high = keep.tile([P, 2 * P * PACK], BF16, name="w_high", align_bytes=64)
-        high_view = w_high[:].rearrange("p (e m j) -> p m j e", e=2, j=PACK)
-        for c in range(2):
-            deal(high_view[:, c * HALF_P : (c + 1) * HALF_P], c, 2)
+        nc.scalar.copy(w_high[:].rearrange("p (e c m j) -> p c m j e", e=2, c=2, j=PACK), w_cols[:, :, :, :, 2:])
         codes_high, plane_high = quantise("w_high", w_high[:], 2 * P)
         for e in range(2):
             bank = psum.tile([P, S], F32, name=f"bank_high{e}")
@@ -198,13 +194,12 @@ def tile_picked_lapl_none_e_kernel(
 
         last = PACK - 1
         fetch(first, last, pos1_sb, gate_sb[0][:], MULT)
-        fetch(second, last, pos2_sb, minus_gate[:], MULT, 0)
+        fetch(second, last, pos2_sb, minus_gate[:], MULT)
         fetch(rest, last, cen_sb, first[:, last, :], SUB, 0)
-        fetch(second, last, pos2_sb, minus_gate[:], MULT, 1)
-        finish(0)
         fetch(rest, last, cen_sb, first[:, last, :], SUB, 1)
-        z_codes0, z_plane0 = quantise("z0", z[0][:], HALF_V)
+        finish(0)
         finish(1)
+        z_codes0, z_plane0 = quantise("z0", z[0][:], HALF_V)
         z_codes1, z_plane1 = quantise("z1", z[1][:], HALF_V)
 
         out_rows = out.rearrange("(m p) v -> p m v", p=P)

@@ -16,7 +16,6 @@ FP8X4 = mybir.dt.float8_e4m3fn_x4
 FP4X4 = mybir.dt.float4_e2m1fn_x4
 MULT = mybir.AluOpType.mult
 ADD = mybir.AluOpType.add
-SUB = mybir.AluOpType.subtract
 
 P = 128
 PACK = 4
@@ -39,7 +38,7 @@ def tile_picked_lapl_none_e_kernel(
         cen_sb = keep.tile([P, V // LIST], U16, name="cen_sb")
         pos1_sb = keep.tile([P, V // LIST], U16, name="pos1_sb")
         pos2_sb = keep.tile([P, V // LIST], U16, name="pos2_sb")
-        gate_sb = [keep.tile([P, V], F32, name=f"gate_sb{d}") for d in range(2)]
+        gate_sb = keep.tile([P, 2, V], F32, name="gate_sb")
         w2_codes = keep.tile([P, 2 * N], U8, name="w2_codes", align_bytes=64)
         w2_plane = keep.tile([P, N], U8, name="w2_plane", align_bytes=64)
         nc.gpsimd.memset(w2_plane[:], 0)
@@ -57,12 +56,11 @@ def tile_picked_lapl_none_e_kernel(
                     nc.sync.dma_start(offs_sb[:], offs)
         w_raw = keep.tile([P, 2, PACK, HALF_H], F32, name="w_raw")
         nc.sync.dma_start(w_raw[:, 0], w_rows[:, :, :HALF_H])
-        nc.sync.dma_start(gate_sb[1][:], gate[1])
         nc.sync.dma_start(w_raw[:, 1], w_rows[:, :, HALF_H:])
-        nc.sync.dma_start(pos1_sb[:], pos1)
-        nc.sync.dma_start(gate_sb[0][:], gate[0])
-        nc.sync.dma_start(pos2_sb[:], pos2)
         nc.sync.dma_start(cen_sb[:], cen)
+        nc.sync.dma_start(gate_sb[:], gate.rearrange("d p v -> p d v"))
+        nc.sync.dma_start(pos1_sb[:], pos1)
+        nc.sync.dma_start(pos2_sb[:], pos2)
         nc.sync.dma_start(w2_codes[:].bitcast(I32), w2_words[0].bitcast(I32))
         for q in range(4):
             nc.sync.dma_start(
@@ -122,10 +120,9 @@ def tile_picked_lapl_none_e_kernel(
             project(bank[:], codes0[:], plane0[:], lo, hi)
             nc.vector.tensor_copy(h_sb[0][:, lo:hi], bank[:])
 
-        minus_gate = keep.tile([P, V], F32, name="minus_gate")
-        nc.scalar.mul(minus_gate[:], gate_sb[1][:], -1.0)
-
         codes1, plane1 = low_weights(1)
+        minus_gate = keep.tile([P, 2, V], F32, name="minus_gate")
+        nc.scalar.mul(minus_gate[:], gate_sb[:], -1.0)
         bank_c = psum.tile([P, S], F32, name="bank_low1")
         project(bank_c[:], codes1[:], plane1[:], 0, S)
         nc.scalar.copy(h_sb[1][:], bank_c[:])
@@ -148,29 +145,33 @@ def tile_picked_lapl_none_e_kernel(
             nc.vector.tensor_tensor(dst[:, n, cols], window, other[:, cols], op)
 
         z = [keep.tile([P, HALF_V * PACK], BF16, name=f"z{c}", align_bytes=64) for c in range(2)]
-        turned = psum.tile([P, 2, 2, P], F32, name="turned")
-        back = psum.tile([P, 2, HALF_V], F32, name="back")
+        turned = [psum.tile([P, 2, P], F32, name=f"turned{c}", tag=tag) for c, tag in enumerate(("bank_a", "bank_b"))]
+        back = [psum.tile([P, HALF_V], F32, name=f"back{c}") for c in range(2)]
 
-        for n in range(PACK - 1):
-            fetch(first, n, pos1_sb, gate_sb[0][:], MULT)
-            fetch(second, n, pos2_sb, minus_gate[:], MULT)
-            fetch(rest, n, cen_sb, first[:, n, :], SUB)
-            if n < 2:
-                for c in range(2):
-                    cols = slice(c * HALF_V, (c + 1) * HALF_V)
-                    for term, begin in ((second, True), (rest, False)):
-                        nc.tensor.matmul(
-                            turned[:, c, n, :], term[:, n, cols], ident[:], start=begin, stop=not begin, is_transpose=True
-                        )
-            if n == 1:
-                for c in range(2):
-                    rows = keep.tile([P, 2 * P], BF16, name=f"z_rows{c}")
-                    nc.scalar.copy(
-                        rows[:].rearrange("v (g m e) -> v g m e", g=2, e=2),
-                        turned[:, c].rearrange("v g (e m) -> v g m e", e=2),
-                    )
-                    nc.tensor.transpose(back[:, c, :], rows[:].bitcast(F32), ident[:])
-                    nc.scalar.copy(z[c][:].bitcast(F32).rearrange("p (v u) -> p v u", u=2)[:, :, 0], back[:, c, :])
+        def turn(term, n, begin, end):
+            for c in range(2):
+                src = term[:, n, c * HALF_V : (c + 1) * HALF_V]
+                nc.tensor.matmul(turned[c][:, n, :], src, ident[:], start=begin, stop=end, is_transpose=True)
+
+        for n in range(2):
+            nc.vector.tensor_copy(rest[:, n, :], h_sb[n][:].indirect(cen_sb[:]))
+            turn(rest, n, True, False)
+            fetch(first, n, pos1_sb, minus_gate[:, 0, :], MULT)
+            turn(first, n, False, False)
+            fetch(second, n, pos2_sb, minus_gate[:, 1, :], MULT)
+            turn(second, n, False, True)
+        for c in range(2):
+            rows = keep.tile([P, 2 * P], BF16, name=f"z_rows{c}")
+            nc.scalar.copy(
+                rows[:].rearrange("v (g m e) -> v g m e", g=2, e=2),
+                turned[c][:].rearrange("v g (e m) -> v g m e", e=2),
+            )
+            nc.tensor.transpose(back[c][:], rows[:].bitcast(F32), ident[:])
+            nc.scalar.copy(z[c][:].bitcast(F32).rearrange("p (v u) -> p v u", u=2)[:, :, 0], back[c][:])
+
+        fetch(first, 2, pos1_sb, minus_gate[:, 0, :], MULT)
+        fetch(second, 2, pos2_sb, minus_gate[:, 1, :], MULT)
+        fetch(rest, 2, cen_sb, first[:, 2, :], ADD)
 
         def finish(c):
             cols = slice(c * HALF_V, (c + 1) * HALF_V)
@@ -193,10 +194,10 @@ def tile_picked_lapl_none_e_kernel(
             )
 
         last = PACK - 1
-        fetch(first, last, pos1_sb, gate_sb[0][:], MULT)
-        fetch(second, last, pos2_sb, minus_gate[:], MULT)
-        fetch(rest, last, cen_sb, first[:, last, :], SUB, 0)
-        fetch(rest, last, cen_sb, first[:, last, :], SUB, 1)
+        fetch(first, last, pos1_sb, minus_gate[:, 0, :], MULT)
+        fetch(second, last, pos2_sb, minus_gate[:, 1, :], MULT)
+        fetch(rest, last, cen_sb, first[:, last, :], ADD, 0)
+        fetch(rest, last, cen_sb, first[:, last, :], ADD, 1)
         finish(0)
         finish(1)
         z_codes0, z_plane0 = quantise("z0", z[0][:], HALF_V)

@@ -22,8 +22,10 @@ PACK = 4
 LIST = 16
 HALF_H = H // 2
 HALF_V = V // 2
-X_LOADS = (((0, 640, 640), (640, 1024, 1024)), ((0, 512, 0), (512, 768, 768), (768, 1024, 928)))
-PICK_PARTS = ((0, 256), (256, 384), (384, 512))
+X_LOADS = (((0, 512, 512), (512, 1024, 864)), ((0, 512, 0), (512, 768, 768), (768, 1024, 928)))
+GATHER_PARTS = (((0, 512),), ((0, 256), (256, 512)))
+PART = 128
+HALF_S = S // 2
 
 
 def tile_picked_lapl_none_e_kernel(
@@ -38,7 +40,8 @@ def tile_picked_lapl_none_e_kernel(
         cen_sb = keep.tile([P, V // LIST], U16, name="cen_sb")
         pos1_sb = keep.tile([P, V // LIST], U16, name="pos1_sb")
         pos2_sb = keep.tile([P, V // LIST], U16, name="pos2_sb")
-        gate_sb = keep.tile([P, 2, V], F32, name="gate_sb")
+        gate_cols = keep.tile([P, 2, 2], F32, name="gate_cols")
+        nc.scalar.dma_start(gate_cols[:], gate[:, 0, :].rearrange("d (p e) -> p d e", e=2))
         w2_codes = keep.tile([P, 2 * N], U8, name="w2_codes", align_bytes=64)
         w2_plane = keep.tile([P, N], U8, name="w2_plane", align_bytes=64)
         nc.gpsimd.memset(w2_plane[:], 0)
@@ -57,19 +60,25 @@ def tile_picked_lapl_none_e_kernel(
         w_raw = keep.tile([P, 2, PACK, HALF_H], F32, name="w_raw")
         nc.sync.dma_start(w_raw[:, 0], w_rows[:, :, :HALF_H])
         nc.sync.dma_start(w_raw[:, 1], w_rows[:, :, HALF_H:])
+        nc.sync.dma_start(w2_codes[:].bitcast(I32), w2_words[0].bitcast(I32))
         nc.sync.dma_start(cen_sb[:], cen)
-        nc.sync.dma_start(gate_sb[:], gate.rearrange("d p v -> p d v"))
         nc.sync.dma_start(pos1_sb[:], pos1)
         nc.sync.dma_start(pos2_sb[:], pos2)
-        nc.sync.dma_start(w2_codes[:].bitcast(I32), w2_words[0].bitcast(I32))
         for q in range(4):
             nc.sync.dma_start(
                 w2_plane[32 * q : 32 * q + 4, :].bitcast(I32), w2_scales[0, 4 * q : 4 * q + 4, :].bitcast(I32)
             )
 
+        minus_cols = keep.tile([P, 2, 2], F32, name="minus_cols")
+        nc.scalar.mul(minus_cols[:], gate_cols[:], -1.0)
+        spread = psum.tile([P, 2, 2, P], F32, name="spread", tag="back0")
+        for d in range(2):
+            for e in range(2):
+                nc.tensor.transpose(spread[:, d, e, :], minus_cols[:, d, e : e + 1].to_broadcast([P, P]), ident[:])
+
         x_pick = keep.tile([P, S * PACK], BF16, name="x_pick", align_bytes=64)
         for u in range(2):
-            pairs = keep.tile([P, T * 2], BF16, name=f"x_pairs{u}")
+            pairs = keep.tile([P, T * 2], BF16, name=f"x_pairs{u}", tag=f"x_pairs{u}", align_bytes=64)
             for base, end, cut in X_LOADS[u]:
                 for lo, hi, copy in ((base, cut, nc.vector.tensor_copy), (cut, end, nc.scalar.copy)):
                     if hi > lo:
@@ -77,15 +86,16 @@ def tile_picked_lapl_none_e_kernel(
                             pairs[:, 2 * lo : 2 * hi].rearrange("p (a i e) -> p a e i", i=4, e=2),
                             x_raw[u, base][:, :, lo - base : hi - base].rearrange("p e (a i) -> p a e i", i=4),
                         )
-            nc.vector.tensor_copy(
-                x_pick[:].bitcast(U32).rearrange("p (s u) -> p s u", u=2)[:, :, u],
-                pairs[:].bitcast(U32).indirect(offs_sb[:]),
-            )
+            for lo, hi in GATHER_PARTS[u]:
+                nc.vector.tensor_copy(
+                    x_pick[:].bitcast(U32).rearrange("p (s u) -> p s u", u=2)[:, lo:hi, u],
+                    pairs[:].bitcast(U32).indirect(offs_sb[:, lo // LIST : hi // LIST]),
+                )
 
         w_cols = w_raw[:].rearrange("p c j (m t) -> p c m j t", t=PACK)
 
-        def quantise(name, src, width):
-            codes = keep.tile([P, width], U32, name=f"{name}_codes", align_bytes=64)
+        def quantise(name, src, width, tag=None):
+            codes = keep.tile([P, width], U32, name=f"{name}_codes", tag=tag or f"{name}_codes", align_bytes=64)
             plane = keep.tile([P, width], U8, name=f"{name}_plane", align_bytes=64)
             nc.vector.quantize_mx(out=codes[:].bitcast(FP8X4), scales=plane[:], in_=src)
             return codes, plane
@@ -93,47 +103,55 @@ def tile_picked_lapl_none_e_kernel(
         def low_weights(c):
             dealt = keep.tile([P, P * PACK], BF16, name=f"w_low{c}", tag=f"w_low{c}", align_bytes=64)
             nc.scalar.copy(dealt[:].rearrange("p (e m j) -> p m j e", e=2, j=PACK), w_cols[:, c, :, :, :2])
-            return quantise(f"w_low{c}", dealt[:], P)
+            return quantise(f"w_low{c}", dealt[:], P, "x_pairs1")
 
-        codes0, plane0 = low_weights(0)
-        x_codes = keep.tile([P, S], U32, name="x_codes", tag="w_low0", align_bytes=64)
-        x_plane = keep.tile([P, S], U8, name="x_plane", align_bytes=64)
+        x_codes, x_plane = [], []
+
+        def quantise_picked(half, tag):
+            x_codes.append(keep.tile([P, HALF_S], U32, name=f"x_codes{half}", tag=tag, align_bytes=64))
+            x_plane.append(keep.tile([P, HALF_S], U8, name=f"x_plane{half}", align_bytes=64))
+            for lo in range(0, HALF_S, PART):
+                first_col = PACK * (half * HALF_S + lo)
+                nc.vector.quantize_mx(
+                    out=x_codes[half][:, lo : lo + PART].bitcast(FP8X4),
+                    scales=x_plane[half][:, lo : lo + PART],
+                    in_=x_pick[:, first_col : first_col + PACK * PART],
+                )
 
         def project(acc, codes, plane, lo, hi):
-            nc.tensor.matmul_mx(
-                out=acc,
-                lhsT=codes.bitcast(FP8X4),
-                lhsT_scale=plane,
-                rhs=x_codes[:, lo:hi].bitcast(FP8X4),
-                rhs_scale=x_plane[:, lo:hi],
-                start=True,
-                stop=True,
-            )
+            for half in range(lo // HALF_S, (hi - 1) // HALF_S + 1):
+                a, b = max(lo, half * HALF_S), min(hi, (half + 1) * HALF_S)
+                cols = slice(a - half * HALF_S, b - half * HALF_S)
+                nc.tensor.matmul_mx(
+                    out=acc[:, a - lo : b - lo],
+                    lhsT=codes.bitcast(FP8X4),
+                    lhsT_scale=plane,
+                    rhs=x_codes[half][:, cols].bitcast(FP8X4),
+                    rhs_scale=x_plane[half][:, cols],
+                    start=True,
+                    stop=True,
+                )
 
         h_sb = [keep.tile([P, S], F32, name=f"h_sb{n}") for n in range(PACK)]
-        for lo, hi in PICK_PARTS:
-            nc.vector.quantize_mx(
-                out=x_codes[:, lo:hi].bitcast(FP8X4), scales=x_plane[:, lo:hi], in_=x_pick[:, PACK * lo : PACK * hi]
-            )
-        for tag, (lo, hi) in zip(("bank_a", "bank_b", "bank_c"), PICK_PARTS):
-            bank = psum.tile([P, hi - lo], F32, name=f"h_part{lo}", tag=tag)
-            project(bank[:], codes0[:], plane0[:], lo, hi)
-            nc.vector.tensor_copy(h_sb[0][:, lo:hi], bank[:])
+        quantise_picked(0, "x_codes0")
+        codes0, plane0 = low_weights(0)
+        quantise_picked(1, "w_low0")
+        for tag, lo in zip(("bank_a", "bank_b", "bank_c", "back1"), range(0, S, PART)):
+            bank = psum.tile([P, PART], F32, name=f"h_part{lo}", tag=tag)
+            project(bank[:], codes0[:], plane0[:], lo, lo + PART)
+            nc.vector.tensor_copy(h_sb[0][:, lo : lo + PART], bank[:])
 
-        codes1, plane1 = low_weights(1)
         minus_gate = keep.tile([P, 2, V], F32, name="minus_gate")
-        nc.scalar.mul(minus_gate[:], gate_sb[:], -1.0)
+        nc.scalar.copy(
+            minus_gate[:].rearrange("p d (n e) -> p d n e", e=2), spread[:].rearrange("p d e n -> p d n e")
+        )
+        codes1, plane1 = low_weights(1)
+        w_high = keep.tile([P, 2 * P * PACK], BF16, name="w_high", align_bytes=64)
+        nc.scalar.copy(w_high[:].rearrange("p (e c m j) -> p c m j e", e=2, c=2, j=PACK), w_cols[:, :, :, :, 2:])
         bank_c = psum.tile([P, S], F32, name="bank_low1")
         project(bank_c[:], codes1[:], plane1[:], 0, S)
         nc.scalar.copy(h_sb[1][:], bank_c[:])
 
-        w_high = keep.tile([P, 2 * P * PACK], BF16, name="w_high", align_bytes=64)
-        nc.scalar.copy(w_high[:].rearrange("p (e c m j) -> p c m j e", e=2, c=2, j=PACK), w_cols[:, :, :, :, 2:])
-        codes_high, plane_high = quantise("w_high", w_high[:], 2 * P)
-        for e in range(2):
-            bank = psum.tile([P, S], F32, name=f"bank_high{e}")
-            project(bank[:], codes_high[:, e * P : (e + 1) * P], plane_high[:, e * P : (e + 1) * P], 0, S)
-            nc.scalar.copy(h_sb[2 + e][:], bank[:])
 
         first = keep.tile([P, PACK, V], F32, name="first")
         second = keep.tile([P, PACK, V], F32, name="second")
@@ -146,20 +164,27 @@ def tile_picked_lapl_none_e_kernel(
 
         z = [keep.tile([P, HALF_V * PACK], BF16, name=f"z{c}", align_bytes=64) for c in range(2)]
         turned = [psum.tile([P, 2, P], F32, name=f"turned{c}", tag=tag) for c, tag in enumerate(("bank_a", "bank_b"))]
-        back = [psum.tile([P, HALF_V], F32, name=f"back{c}") for c in range(2)]
+        back = [psum.tile([P, HALF_V], F32, name=f"back{c}", tag=f"back{c}") for c in range(2)]
 
         def turn(term, n, begin, end):
             for c in range(2):
-                src = term[:, n, c * HALF_V : (c + 1) * HALF_V]
+                src = term[:, c * HALF_V : (c + 1) * HALF_V]
                 nc.tensor.matmul(turned[c][:, n, :], src, ident[:], start=begin, stop=end, is_transpose=True)
 
         for n in range(2):
-            nc.vector.tensor_copy(rest[:, n, :], h_sb[n][:].indirect(cen_sb[:]))
-            turn(rest, n, True, False)
+            centre = keep.tile([P, V], F32, name=f"centre{n}", tag=f"centre{n}", align_bytes=64)
+            nc.vector.tensor_copy(centre[:], h_sb[n][:].indirect(cen_sb[:]))
+            turn(centre, n, True, False)
             fetch(first, n, pos1_sb, minus_gate[:, 0, :], MULT)
-            turn(first, n, False, False)
+            turn(first[:, n, :], n, False, False)
+            if n == 0:
+                codes_high, plane_high = quantise("w_high", w_high[:], 2 * P, "w_low1")
+                for e in range(2):
+                    bank = psum.tile([P, S], F32, name=f"bank_high{e}")
+                    project(bank[:], codes_high[:, e * P : (e + 1) * P], plane_high[:, e * P : (e + 1) * P], 0, S)
+                    nc.scalar.copy(h_sb[2 + e][:], bank[:])
             fetch(second, n, pos2_sb, minus_gate[:, 1, :], MULT)
-            turn(second, n, False, True)
+            turn(second[:, n, :], n, False, True)
         for c in range(2):
             rows = keep.tile([P, 2 * P], BF16, name=f"z_rows{c}")
             nc.scalar.copy(

@@ -22,7 +22,7 @@ PACK = 4
 LIST = 16
 HALF_H = H // 2
 HALF_V = V // 2
-X_LOADS = (((0, 512, 512), (512, 1024, 864)), ((0, 512, 0), (512, 768, 768), (768, 1024, 928)))
+X_LOADS = (((0, 768, 512), (768, 1024, 936)), ((0, 512, 0), (512, 768, 768), (768, 1024, 928)))
 GATHER_PARTS = (((0, 512),), ((0, 256), (256, 512)))
 PART = 128
 HALF_S = S // 2
@@ -40,8 +40,9 @@ def tile_picked_lapl_none_e_kernel(
         cen_sb = keep.tile([P, V // LIST], U16, name="cen_sb")
         pos1_sb = keep.tile([P, V // LIST], U16, name="pos1_sb")
         pos2_sb = keep.tile([P, V // LIST], U16, name="pos2_sb")
-        gate_cols = keep.tile([P, 2, 2], F32, name="gate_cols")
-        nc.scalar.dma_start(gate_cols[:], gate[:, 0, :].rearrange("d (p e) -> p d e", e=2))
+        both_rows = gate.rearrange("d p v -> (d p v)")[(P - 1) * V : (P + 1) * V]
+        gate_cols = keep.tile([P, PACK], F32, name="gate_cols")
+        nc.scalar.dma_start(gate_cols[:], both_rows.rearrange("(p e) -> p e", e=PACK))
         w2_codes = keep.tile([P, 2 * N], U8, name="w2_codes", align_bytes=64)
         w2_plane = keep.tile([P, N], U8, name="w2_plane", align_bytes=64)
         nc.gpsimd.memset(w2_plane[:], 0)
@@ -53,7 +54,7 @@ def tile_picked_lapl_none_e_kernel(
         x_raw = {}
         for u in range(2):
             for lo, hi, cut in X_LOADS[u]:
-                x_raw[u, lo] = keep.tile([P, 2, hi - lo], F32, name=f"x_raw{u}_{lo}")
+                x_raw[u, lo] = keep.tile([P, 2, hi - lo], F32, name=f"x_raw{u}_{lo}", tag=f"x_raw{u}_{lo}")
                 nc.sync.dma_start(x_raw[u, lo][:], x_rows[:, 2 * u : 2 * u + 2, lo:hi])
                 if (u, lo) == (0, 0):
                     nc.sync.dma_start(offs_sb[:], offs)
@@ -69,12 +70,11 @@ def tile_picked_lapl_none_e_kernel(
                 w2_plane[32 * q : 32 * q + 4, :].bitcast(I32), w2_scales[0, 4 * q : 4 * q + 4, :].bitcast(I32)
             )
 
-        minus_cols = keep.tile([P, 2, 2], F32, name="minus_cols")
+        minus_cols = keep.tile([P, PACK], F32, name="minus_cols")
         nc.scalar.mul(minus_cols[:], gate_cols[:], -1.0)
-        spread = psum.tile([P, 2, 2, P], F32, name="spread", tag="back0")
-        for d in range(2):
-            for e in range(2):
-                nc.tensor.transpose(spread[:, d, e, :], minus_cols[:, d, e : e + 1].to_broadcast([P, P]), ident[:])
+        spread = psum.tile([P, PACK, P], F32, name="spread", tag="back0")
+        for e in range(PACK):
+            nc.tensor.transpose(spread[:, e, :], minus_cols[:, e : e + 1].to_broadcast([P, P]), ident[:])
 
         x_pick = keep.tile([P, S * PACK], BF16, name="x_pick", align_bytes=64)
         for u in range(2):
@@ -141,9 +141,9 @@ def tile_picked_lapl_none_e_kernel(
             project(bank[:], codes0[:], plane0[:], lo, lo + PART)
             nc.vector.tensor_copy(h_sb[0][:, lo : lo + PART], bank[:])
 
-        minus_gate = keep.tile([P, 2, V], F32, name="minus_gate")
+        minus_gate = keep.tile([P, 2, V], F32, name="minus_gate", tag="x_raw1_768")
         nc.scalar.copy(
-            minus_gate[:].rearrange("p d (n e) -> p d n e", e=2), spread[:].rearrange("p d e n -> p d n e")
+            minus_gate[:].rearrange("p d (n e) -> p (d n) e", e=PACK), spread[:].rearrange("p e n -> p n e")
         )
         codes1, plane1 = low_weights(1)
         w_high = keep.tile([P, 2 * P * PACK], BF16, name="w_high", align_bytes=64)

@@ -22,8 +22,8 @@ PACK = 4
 LIST = 16
 HALF_H = H // 2
 HALF_V = V // 2
-X_LOADS = (((0, 768, 512), (768, 1024, 936)), ((0, 512, 0), (512, 768, 768), (768, 1024, 928)))
-GATHER_PARTS = (((0, 512),), ((0, 256), (256, 512)))
+X_LOADS = (((0, 768, 512), (768, 1024, 936)), ((0, 512, 64), (512, 768, 768), (768, 1024, 944)))
+GATHER_PARTS = (((0, 512),), ((0, 128), (128, 384), (384, 512)))
 PART = 128
 HALF_S = S // 2
 
@@ -77,6 +77,7 @@ def tile_picked_lapl_none_e_kernel(
             nc.tensor.transpose(spread[:, e, :], minus_cols[:, e : e + 1].to_broadcast([P, P]), ident[:])
 
         x_pick = keep.tile([P, S * PACK], BF16, name="x_pick", align_bytes=64)
+        picked = keep.tile([P, 2, S], U32, name="picked")
         for u in range(2):
             pairs = keep.tile([P, T * 2], BF16, name=f"x_pairs{u}", tag=f"x_pairs{u}", align_bytes=64)
             for base, end, cut in X_LOADS[u]:
@@ -88,10 +89,16 @@ def tile_picked_lapl_none_e_kernel(
                         )
             for lo, hi in GATHER_PARTS[u]:
                 nc.vector.tensor_copy(
-                    x_pick[:].bitcast(U32).rearrange("p (s u) -> p s u", u=2)[:, lo:hi, u],
+                    picked[:, u, lo:hi],
                     pairs[:].bitcast(U32).indirect(offs_sb[:, lo // LIST : hi // LIST]),
                 )
 
+        for lo, hi in GATHER_PARTS[1]:
+            copy, word = (nc.vector.tensor_copy, I32) if lo else (nc.scalar.copy, U32)
+            copy(
+                x_pick[:].bitcast(word).rearrange("p (s u) -> p s u", u=2)[:, lo:hi, :],
+                picked[:, :, lo:hi].bitcast(word).rearrange("p u s -> p s u"),
+            )
         w_cols = w_raw[:].rearrange("p c j (m t) -> p c m j t", t=PACK)
 
         def quantise(name, src, width, tag=None):
@@ -141,7 +148,7 @@ def tile_picked_lapl_none_e_kernel(
             project(bank[:], codes0[:], plane0[:], lo, lo + PART)
             nc.vector.tensor_copy(h_sb[0][:, lo : lo + PART], bank[:])
 
-        minus_gate = keep.tile([P, 2, V], F32, name="minus_gate", tag="x_raw1_768")
+        minus_gate = keep.tile([P, 2, V], F32, name="minus_gate")
         nc.scalar.copy(
             minus_gate[:].rearrange("p d (n e) -> p (d n) e", e=PACK), spread[:].rearrange("p e n -> p n e")
         )

@@ -58,9 +58,9 @@ def tile_picked_lapl_none_e_kernel(
                 nc.sync.dma_start(x_raw[u, lo][:], x_rows[:, 2 * u : 2 * u + 2, lo:hi])
                 if (u, lo) == (0, 0):
                     nc.sync.dma_start(offs_sb[:], offs)
-        w_raw = keep.tile([P, 2, PACK, HALF_H], F32, name="w_raw")
-        nc.sync.dma_start(w_raw[:, 0], w_rows[:, :, :HALF_H])
-        nc.sync.dma_start(w_raw[:, 1], w_rows[:, :, HALF_H:])
+        w_raw = keep.tile([P, 4, PACK, P], F32, name="w_raw")
+        for quarter in range(4):
+            nc.sync.dma_start(w_raw[:, quarter], w_rows[:, :, quarter * P : (quarter + 1) * P])
         nc.sync.dma_start(w2_codes[:].bitcast(I32), w2_words[0].bitcast(I32))
         nc.sync.dma_start(cen_sb[:], cen)
         nc.sync.dma_start(pos1_sb[:], pos1)
@@ -99,7 +99,7 @@ def tile_picked_lapl_none_e_kernel(
                 x_pick[:].bitcast(word).rearrange("p (s u) -> p s u", u=2)[:, lo:hi, :],
                 picked[:, :, lo:hi].bitcast(word).rearrange("p u s -> p s u"),
             )
-        w_cols = w_raw[:].rearrange("p c j (m t) -> p c m j t", t=PACK)
+        w_cols = w_raw[:].rearrange("p q j (m t) -> p q m j t", t=PACK)
 
         def quantise(name, src, width, tag=None):
             codes = keep.tile([P, width], U32, name=f"{name}_codes", tag=tag or f"{name}_codes", align_bytes=64)
@@ -109,40 +109,41 @@ def tile_picked_lapl_none_e_kernel(
 
         def low_weights(c):
             dealt = keep.tile([P, P * PACK], BF16, name=f"w_low{c}", tag=f"w_low{c}", align_bytes=64)
-            nc.scalar.copy(dealt[:].rearrange("p (e m j) -> p m j e", e=2, j=PACK), w_cols[:, c, :, :, :2])
+            view = dealt[:].rearrange("p (q m e j) -> p q m j e", q=2, e=2, j=PACK)
+            for q in (slice(0, 2),) if c else (slice(0, 1), slice(1, 2)):
+                nc.scalar.copy(view[:, q], w_cols[:, 2 * c : 2 * c + 2][:, q, :, :, :2])
             return quantise(f"w_low{c}", dealt[:], P, "x_pairs1")
 
-        x_codes, x_plane = [], []
+        x_codes, x_plane = {}, {}
 
-        def quantise_picked(half, tag):
-            x_codes.append(keep.tile([P, HALF_S], U32, name=f"x_codes{half}", tag=tag, align_bytes=64))
-            x_plane.append(keep.tile([P, HALF_S], U8, name=f"x_plane{half}", align_bytes=64))
-            for lo in range(0, HALF_S, PART):
-                first_col = PACK * (half * HALF_S + lo)
+        def quantise_picked(base, end, tag):
+            codes = keep.tile([P, end - base], U32, name=f"x_codes{base}", tag=tag, align_bytes=64)
+            plane = keep.tile([P, end - base], U8, name=f"x_plane{base}", align_bytes=64)
+            for lo in range(0, end - base, PART):
+                x_codes[base + lo], x_plane[base + lo] = codes[:, lo:], plane[:, lo:]
+                first_col = PACK * (base + lo)
                 nc.vector.quantize_mx(
-                    out=x_codes[half][:, lo : lo + PART].bitcast(FP8X4),
-                    scales=x_plane[half][:, lo : lo + PART],
+                    out=codes[:, lo : lo + PART].bitcast(FP8X4),
+                    scales=plane[:, lo : lo + PART],
                     in_=x_pick[:, first_col : first_col + PACK * PART],
                 )
 
         def project(acc, codes, plane, lo, hi):
-            for half in range(lo // HALF_S, (hi - 1) // HALF_S + 1):
-                a, b = max(lo, half * HALF_S), min(hi, (half + 1) * HALF_S)
-                cols = slice(a - half * HALF_S, b - half * HALF_S)
+            for a, b in ((0, 128), (128, 384), (384, 512)) if hi - lo == S else ((lo, hi),):
                 nc.tensor.matmul_mx(
                     out=acc[:, a - lo : b - lo],
                     lhsT=codes.bitcast(FP8X4),
                     lhsT_scale=plane,
-                    rhs=x_codes[half][:, cols].bitcast(FP8X4),
-                    rhs_scale=x_plane[half][:, cols],
+                    rhs=x_codes[a][:, : b - a].bitcast(FP8X4),
+                    rhs_scale=x_plane[a][:, : b - a],
                     start=True,
                     stop=True,
                 )
 
         h_sb = [keep.tile([P, S], F32, name=f"h_sb{n}") for n in range(PACK)]
-        quantise_picked(0, "x_codes0")
+        quantise_picked(0, PART, "x_codes0")
         codes0, plane0 = low_weights(0)
-        quantise_picked(1, "w_low0")
+        quantise_picked(PART, S, "w_low0")
         for tag, lo in zip(("bank_a", "bank_b", "bank_c", "back1"), range(0, S, PART)):
             bank = psum.tile([P, PART], F32, name=f"h_part{lo}", tag=tag)
             project(bank[:], codes0[:], plane0[:], lo, lo + PART)
@@ -154,7 +155,7 @@ def tile_picked_lapl_none_e_kernel(
         )
         codes1, plane1 = low_weights(1)
         w_high = keep.tile([P, 2 * P * PACK], BF16, name="w_high", align_bytes=64)
-        nc.scalar.copy(w_high[:].rearrange("p (e c m j) -> p c m j e", e=2, c=2, j=PACK), w_cols[:, :, :, :, 2:])
+        nc.scalar.copy(w_high[:].rearrange("p (e q m j) -> p q m j e", e=2, q=4, j=PACK), w_cols[:, :, :, :, 2:])
         bank_c = psum.tile([P, S], F32, name="bank_low1")
         project(bank_c[:], codes1[:], plane1[:], 0, S)
         nc.scalar.copy(h_sb[1][:], bank_c[:])
@@ -194,10 +195,7 @@ def tile_picked_lapl_none_e_kernel(
             turn(second[:, n, :], n, False, True)
         for c in range(2):
             rows = keep.tile([P, 2 * P], BF16, name=f"z_rows{c}")
-            nc.scalar.copy(
-                rows[:].rearrange("v (g m e) -> v g m e", g=2, e=2),
-                turned[c][:].rearrange("v g (e m) -> v g m e", e=2),
-            )
+            nc.scalar.copy(rows[:], turned[c][:].rearrange("v g q -> v (g q)"))
             nc.tensor.transpose(back[c][:], rows[:].bitcast(F32), ident[:])
             nc.scalar.copy(z[c][:].bitcast(F32).rearrange("p (v u) -> p v u", u=2)[:, :, 0], back[c][:])
 

@@ -22,7 +22,7 @@ PACK = 4
 LIST = 16
 HALF_H = H // 2
 HALF_V = V // 2
-X_LOADS = (((0, 768, 512), (768, 1024, 936)), ((0, 512, 64), (512, 768, 768), (768, 1024, 944)))
+X_LOADS = (((0, 768, 512), (768, 1024, 936)), ((0, 512, 64), (512, 768, 768), (768, 896, 832), (896, 1024, 984)))
 GATHER_PARTS = (((0, 512),), ((0, 128), (128, 384), (384, 512)))
 PART = 128
 HALF_S = S // 2
@@ -58,13 +58,13 @@ def tile_picked_lapl_none_e_kernel(
                 nc.sync.dma_start(x_raw[u, lo][:], x_rows[:, 2 * u : 2 * u + 2, lo:hi])
                 if (u, lo) == (0, 0):
                     nc.sync.dma_start(offs_sb[:], offs)
-        w_raw = keep.tile([P, 4, PACK, P], F32, name="w_raw")
+        w_raw = keep.tile([P, 4, PACK, P], F32, name="w_raw", tag="w_raw")
         for quarter in range(4):
             nc.sync.dma_start(w_raw[:, quarter], w_rows[:, :, quarter * P : (quarter + 1) * P])
-        nc.sync.dma_start(w2_codes[:].bitcast(I32), w2_words[0].bitcast(I32))
-        nc.sync.dma_start(cen_sb[:], cen)
         nc.sync.dma_start(pos1_sb[:], pos1)
+        nc.sync.dma_start(cen_sb[:], cen)
         nc.sync.dma_start(pos2_sb[:], pos2)
+        nc.sync.dma_start(w2_codes[:].bitcast(I32), w2_words[0].bitcast(I32))
         for q in range(4):
             nc.sync.dma_start(
                 w2_plane[32 * q : 32 * q + 4, :].bitcast(I32), w2_scales[0, 4 * q : 4 * q + 4, :].bitcast(I32)
@@ -110,7 +110,7 @@ def tile_picked_lapl_none_e_kernel(
         def low_weights(c):
             dealt = keep.tile([P, P * PACK], BF16, name=f"w_low{c}", tag=f"w_low{c}", align_bytes=64)
             view = dealt[:].rearrange("p (q m e j) -> p q m j e", q=2, e=2, j=PACK)
-            for q in (slice(0, 2),) if c else (slice(0, 1), slice(1, 2)):
+            for q in (slice(0, 1), slice(1, 2)):
                 nc.scalar.copy(view[:, q], w_cols[:, 2 * c : 2 * c + 2][:, q, :, :, :2])
             return quantise(f"w_low{c}", dealt[:], P, "x_pairs1")
 
@@ -149,13 +149,17 @@ def tile_picked_lapl_none_e_kernel(
             project(bank[:], codes0[:], plane0[:], lo, lo + PART)
             nc.vector.tensor_copy(h_sb[0][:, lo : lo + PART], bank[:])
 
-        minus_gate = keep.tile([P, 2, V], F32, name="minus_gate")
+        w_high = keep.tile([P, 2 * P * PACK], BF16, name="w_high", align_bytes=64)
+        high_dealt = w_high[:].rearrange("p (e q m j) -> p q m j e", e=2, q=4, j=PACK)
+        nc.scalar.copy(high_dealt[:, :2], w_cols[:, :2, :, :, 2:])
+        codes1, plane1 = low_weights(1)
+        for q in (2, 3):
+            nc.scalar.copy(high_dealt[:, q : q + 1], w_cols[:, q : q + 1, :, :, 2:])
+        codes_high, plane_high = quantise("w_high", w_high[:], 2 * P)
+        minus_gate = keep.tile([P, 2, V], F32, name="minus_gate", tag="w_raw")
         nc.scalar.copy(
             minus_gate[:].rearrange("p d (n e) -> p (d n) e", e=PACK), spread[:].rearrange("p e n -> p n e")
         )
-        codes1, plane1 = low_weights(1)
-        w_high = keep.tile([P, 2 * P * PACK], BF16, name="w_high", align_bytes=64)
-        nc.scalar.copy(w_high[:].rearrange("p (e q m j) -> p q m j e", e=2, q=4, j=PACK), w_cols[:, :, :, :, 2:])
         bank_c = psum.tile([P, S], F32, name="bank_low1")
         project(bank_c[:], codes1[:], plane1[:], 0, S)
         nc.scalar.copy(h_sb[1][:], bank_c[:])
@@ -186,7 +190,6 @@ def tile_picked_lapl_none_e_kernel(
             fetch(first, n, pos1_sb, minus_gate[:, 0, :], MULT)
             turn(first[:, n, :], n, False, False)
             if n == 0:
-                codes_high, plane_high = quantise("w_high", w_high[:], 2 * P, "w_low1")
                 for e in range(2):
                     bank = psum.tile([P, S], F32, name=f"bank_high{e}")
                     project(bank[:], codes_high[:, e * P : (e + 1) * P], plane_high[:, e * P : (e + 1) * P], 0, S)

@@ -112,7 +112,7 @@ def tile_picked_lapl_none_e_kernel(
             view = dealt[:].rearrange("p (q m e j) -> p q m j e", q=2, e=2, j=PACK)
             for q in (slice(0, 1), slice(1, 2)):
                 nc.scalar.copy(view[:, q], w_cols[:, 2 * c : 2 * c + 2][:, q, :, :, :2])
-            return quantise(f"w_low{c}", dealt[:], P, "x_pairs1")
+            return quantise(f"w_low{c}", dealt[:], P, None if c else "x_pairs1")
 
         x_codes, x_plane = {}, {}
 
@@ -147,7 +147,9 @@ def tile_picked_lapl_none_e_kernel(
         for tag, lo in zip(("bank_a", "bank_b", "bank_c", "back1"), range(0, S, PART)):
             bank = psum.tile([P, PART], F32, name=f"h_part{lo}", tag=tag)
             project(bank[:], codes0[:], plane0[:], lo, lo + PART)
-            nc.vector.tensor_copy(h_sb[0][:, lo : lo + PART], bank[:])
+            if lo < S - PART:
+                nc.vector.tensor_copy(h_sb[0][:, lo : lo + PART], bank[:])
+        last_part = bank
 
         w_high = keep.tile([P, 2 * P * PACK], BF16, name="w_high", align_bytes=64)
         high_dealt = w_high[:].rearrange("p (e q m j) -> p q m j e", e=2, q=4, j=PACK)
@@ -156,10 +158,13 @@ def tile_picked_lapl_none_e_kernel(
         for q in (2, 3):
             nc.scalar.copy(high_dealt[:, q : q + 1], w_cols[:, q : q + 1, :, :, 2:])
         codes_high, plane_high = quantise("w_high", w_high[:], 2 * P)
+        nc.scalar.copy(h_sb[0][:, S - PART :], last_part[:])
         minus_gate = keep.tile([P, 2, V], F32, name="minus_gate", tag="w_raw")
-        nc.scalar.copy(
-            minus_gate[:].rearrange("p d (n e) -> p (d n) e", e=PACK), spread[:].rearrange("p e n -> p n e")
-        )
+        for d in range(2):
+            nc.scalar.copy(
+                minus_gate[:, d, :].rearrange("p (n e) -> p n e", e=PACK),
+                spread[:].rearrange("p e (d n) -> p d n e", d=2)[:, d],
+            )
         bank_c = psum.tile([P, S], F32, name="bank_low1")
         project(bank_c[:], codes1[:], plane1[:], 0, S)
         nc.scalar.copy(h_sb[1][:], bank_c[:])

@@ -58,9 +58,9 @@ def tile_picked_lapl_none_e_kernel(
                 nc.sync.dma_start(x_raw[u, lo][:], x_rows[:, 2 * u : 2 * u + 2, lo:hi])
                 if (u, lo) == (0, 0):
                     nc.sync.dma_start(offs_sb[:], offs)
-        w_raw = keep.tile([P, 4, PACK, P], F32, name="w_raw", tag="w_raw")
+        w_raw = [keep.tile([P, PACK, P], F32, name=f"w_raw{q}", tag=f"w_raw{q}", align_bytes=64) for q in range(4)]
         for quarter in range(4):
-            nc.sync.dma_start(w_raw[:, quarter], w_rows[:, :, quarter * P : (quarter + 1) * P])
+            nc.sync.dma_start(w_raw[quarter][:], w_rows[:, :, quarter * P : (quarter + 1) * P])
         nc.sync.dma_start(pos1_sb[:], pos1)
         nc.sync.dma_start(cen_sb[:], cen)
         nc.sync.dma_start(pos2_sb[:], pos2)
@@ -93,26 +93,32 @@ def tile_picked_lapl_none_e_kernel(
                     pairs[:].bitcast(U32).indirect(offs_sb[:, lo // LIST : hi // LIST]),
                 )
 
+        w_cols = [raw[:].rearrange("p j (m t) -> p m j t", t=PACK) for raw in w_raw]
+        w_high = keep.tile([P, 2 * P * PACK], BF16, name="w_high", align_bytes=64)
+        high_dealt = w_high[:].rearrange("p (e q m j) -> p q m j e", e=2, q=4, j=PACK)
+        low_dealt = [keep.tile([P, P * PACK], BF16, name=f"w_low{c}", tag=f"w_low{c}", align_bytes=64) for c in range(2)]
+
+        def deal_low(q):
+            view = low_dealt[q // 2][:].rearrange("p (q m e j) -> p q m j e", q=2, e=2, j=PACK)
+            nc.scalar.copy(view[:, q % 2], w_cols[q][:, :, :, :2])
+
+        def deal_high(q):
+            nc.scalar.copy(high_dealt[:, q], w_cols[q][:, :, :, 2:])
+
+        deal_low(0)
+        deal_high(0)
         for lo, hi in GATHER_PARTS[1]:
             copy, word = (nc.vector.tensor_copy, I32) if lo else (nc.scalar.copy, U32)
             copy(
                 x_pick[:].bitcast(word).rearrange("p (s u) -> p s u", u=2)[:, lo:hi, :],
                 picked[:, :, lo:hi].bitcast(word).rearrange("p u s -> p s u"),
             )
-        w_cols = w_raw[:].rearrange("p q j (m t) -> p q m j t", t=PACK)
 
         def quantise(name, src, width, tag=None):
             codes = keep.tile([P, width], U32, name=f"{name}_codes", tag=tag or f"{name}_codes", align_bytes=64)
             plane = keep.tile([P, width], U8, name=f"{name}_plane", align_bytes=64)
             nc.vector.quantize_mx(out=codes[:].bitcast(FP8X4), scales=plane[:], in_=src)
             return codes, plane
-
-        def low_weights(c):
-            dealt = keep.tile([P, P * PACK], BF16, name=f"w_low{c}", tag=f"w_low{c}", align_bytes=64)
-            view = dealt[:].rearrange("p (q m e j) -> p q m j e", q=2, e=2, j=PACK)
-            for q in (slice(0, 1), slice(1, 2)):
-                nc.scalar.copy(view[:, q], w_cols[:, 2 * c : 2 * c + 2][:, q, :, :, :2])
-            return quantise(f"w_low{c}", dealt[:], P, None if c else "x_pairs1")
 
         x_codes, x_plane = {}, {}
 
@@ -142,24 +148,28 @@ def tile_picked_lapl_none_e_kernel(
 
         h_sb = [keep.tile([P, S], F32, name=f"h_sb{n}") for n in range(PACK)]
         quantise_picked(0, PART, "x_codes0")
-        codes0, plane0 = low_weights(0)
-        quantise_picked(PART, S, "w_low0")
+        deal_low(1)
+        codes0, plane0 = quantise("w_low0", low_dealt[0][:], P, "x_pairs1")
+        deal_high(1)
+        quantise_picked(PART, S, "w_raw1")
+        late_parts = []
         for tag, lo in zip(("bank_a", "bank_b", "bank_c", "back1"), range(0, S, PART)):
             bank = psum.tile([P, PART], F32, name=f"h_part{lo}", tag=tag)
             project(bank[:], codes0[:], plane0[:], lo, lo + PART)
-            if lo < S - PART:
+            if lo < PART:
                 nc.vector.tensor_copy(h_sb[0][:, lo : lo + PART], bank[:])
-        last_part = bank
+            else:
+                late_parts.append((lo, bank))
 
-        w_high = keep.tile([P, 2 * P * PACK], BF16, name="w_high", align_bytes=64)
-        high_dealt = w_high[:].rearrange("p (e q m j) -> p q m j e", e=2, q=4, j=PACK)
-        nc.scalar.copy(high_dealt[:, :2], w_cols[:, :2, :, :, 2:])
-        codes1, plane1 = low_weights(1)
         for q in (2, 3):
-            nc.scalar.copy(high_dealt[:, q : q + 1], w_cols[:, q : q + 1, :, :, 2:])
+            deal_low(q)
+        codes1, plane1 = quantise("w_low1", low_dealt[1][:], P)
+        for q in (2, 3):
+            deal_high(q)
         codes_high, plane_high = quantise("w_high", w_high[:], 2 * P)
-        nc.scalar.copy(h_sb[0][:, S - PART :], last_part[:])
-        minus_gate = keep.tile([P, 2, V], F32, name="minus_gate", tag="w_raw")
+        for lo, bank in late_parts:
+            nc.scalar.copy(h_sb[0][:, lo : lo + PART], bank[:])
+        minus_gate = keep.tile([P, 2, V], F32, name="minus_gate", tag="w_raw3", align_bytes=64)
         for d in range(2):
             nc.scalar.copy(
                 minus_gate[:, d, :].rearrange("p (n e) -> p n e", e=PACK),

@@ -156,16 +156,15 @@ def tile_picked_lapl_none_e_kernel(
         for tag, lo in zip(("bank_a", "bank_b", "bank_c", "back1"), range(0, S, PART)):
             bank = psum.tile([P, PART], F32, name=f"h_part{lo}", tag=tag)
             project(bank[:], codes0[:], plane0[:], lo, lo + PART)
-            if lo < PART:
+            if lo < S - PART:
                 nc.vector.tensor_copy(h_sb[0][:, lo : lo + PART], bank[:])
             else:
                 late_parts.append((lo, bank))
 
         for q in (2, 3):
             deal_low(q)
-        codes1, plane1 = quantise("w_low1", low_dealt[1][:], P)
-        for q in (2, 3):
             deal_high(q)
+        codes1, plane1 = quantise("w_low1", low_dealt[1][:], P)
         codes_high, plane_high = quantise("w_high", w_high[:], 2 * P)
         for lo, bank in late_parts:
             nc.scalar.copy(h_sb[0][:, lo : lo + PART], bank[:])

@@ -22,7 +22,7 @@ PACK = 4
 LIST = 16
 HALF_H = H // 2
 HALF_V = V // 2
-X_LOADS = (((0, 768, 512), (768, 1024, 936)), ((0, 512, 64), (512, 768, 768), (768, 896, 832), (896, 1024, 984)))
+X_LOADS = (((0, 512, 344), (512, 896, 768), (896, 1024, 984)), ((0, 512, 128), (512, 896, 768), (896, 1024, 984)))
 GATHER_PARTS = (((0, 512),), ((0, 128), (128, 384), (384, 512)))
 PART = 128
 HALF_S = S // 2
@@ -52,12 +52,18 @@ def tile_picked_lapl_none_e_kernel(
         x_rows = xT.rearrange("(p j) t -> p j t", j=PACK)
         w_rows = w1.rearrange("(p j) c -> p j c", j=PACK)
         x_raw = {}
-        for u in range(2):
-            for lo, hi, cut in X_LOADS[u]:
-                x_raw[u, lo] = keep.tile([P, 2, hi - lo], F32, name=f"x_raw{u}_{lo}", tag=f"x_raw{u}_{lo}")
-                nc.sync.dma_start(x_raw[u, lo][:], x_rows[:, 2 * u : 2 * u + 2, lo:hi])
-                if (u, lo) == (0, 0):
-                    nc.sync.dma_start(offs_sb[:], offs)
+        first_rows = keep.tile([P, 2 * T], F32, name="first_rows")
+        first_run = xT.rearrange("(p j) t -> p (j t)", j=PACK)
+        for lo, hi, cut in X_LOADS[0]:
+            run = slice(T + lo if lo else 0, T + hi)
+            nc.sync.dma_start(first_rows[:, run], first_run[:, run])
+            x_raw[0, lo] = first_rows[:].rearrange("p (e t) -> p e t", e=2)[:, :, lo:hi]
+            if lo == 0:
+                nc.sync.dma_start(offs_sb[:], offs)
+        for lo, hi, cut in X_LOADS[1]:
+            piece = keep.tile([P, 2, hi - lo], F32, name=f"x_raw{lo}")
+            nc.sync.dma_start(piece[:], x_rows[:, 2:, lo:hi])
+            x_raw[1, lo] = piece[:]
         w_raw = [keep.tile([P, PACK, P], F32, name=f"w_raw{q}", tag=f"w_raw{q}", align_bytes=64) for q in range(4)]
         for quarter in range(4):
             nc.sync.dma_start(w_raw[quarter][:], w_rows[:, :, quarter * P : (quarter + 1) * P])

@@ -16,16 +16,15 @@ FP8X4 = mybir.dt.float8_e4m3fn_x4
 FP4X4 = mybir.dt.float4_e2m1fn_x4
 MULT = mybir.AluOpType.mult
 ADD = mybir.AluOpType.add
+COPY = mybir.ActivationFunctionType.Copy
 
 P = 128
 PACK = 4
 LIST = 16
+HALF_S = S // 2
 HALF_H = H // 2
 HALF_V = V // 2
-X_LOADS = (((0, 512, 344), (512, 896, 768), (896, 1024, 984)), ((0, 512, 128), (512, 896, 768), (896, 1024, 984)))
-GATHER_PARTS = (((0, 512),), ((0, 128), (128, 384), (384, 512)))
-PART = 128
-HALF_S = S // 2
+RUN = 4
 
 
 def tile_picked_lapl_none_e_kernel(
@@ -51,24 +50,20 @@ def tile_picked_lapl_none_e_kernel(
 
         x_rows = xT.rearrange("(p j) t -> p j t", j=PACK)
         w_rows = w1.rearrange("(p j) c -> p j c", j=PACK)
-        x_raw = {}
-        first_rows = keep.tile([P, 2 * T], F32, name="first_rows")
-        first_run = xT.rearrange("(p j) t -> p (j t)", j=PACK)
-        for lo, hi, cut in X_LOADS[0]:
-            run = slice(T + lo if lo else 0, T + hi)
-            nc.sync.dma_start(first_rows[:, run], first_run[:, run])
-            x_raw[0, lo] = first_rows[:].rearrange("p (e t) -> p e t", e=2)[:, :, lo:hi]
-            if lo == 0:
+        x_row = []
+        for j in range(PACK):
+            row = keep.tile([P, T], F32, name=f"x_row{j}")
+            nc.sync.dma_start(row[:], x_rows[:, j, :])
+            x_row.append(row)
+            if j == 0:
                 nc.sync.dma_start(offs_sb[:], offs)
-        for lo, hi, cut in X_LOADS[1]:
-            piece = keep.tile([P, 2, hi - lo], F32, name=f"x_raw{lo}")
-            nc.sync.dma_start(piece[:], x_rows[:, 2:, lo:hi])
-            x_raw[1, lo] = piece[:]
-        w_raw = [keep.tile([P, PACK, P], F32, name=f"w_raw{q}", tag=f"w_raw{q}", align_bytes=64) for q in range(4)]
-        for quarter in range(4):
-            nc.sync.dma_start(w_raw[quarter][:], w_rows[:, :, quarter * P : (quarter + 1) * P])
-        nc.sync.dma_start(pos1_sb[:], pos1)
+        w_head = keep.tile([P, 2, PACK, P], F32, name="w_head")
+        for q in range(2):
+            nc.sync.dma_start(w_head[:, q], w_rows[:, :, q * P : (q + 1) * P])
+        w_tail = keep.tile([P, PACK, HALF_H], F32, name="w_tail")
+        nc.sync.dma_start(w_tail[:], w_rows[:, :, HALF_H:])
         nc.sync.dma_start(cen_sb[:], cen)
+        nc.sync.dma_start(pos1_sb[:], pos1)
         nc.sync.dma_start(pos2_sb[:], pos2)
         nc.sync.dma_start(w2_codes[:].bitcast(I32), w2_words[0].bitcast(I32))
         for q in range(4):
@@ -78,125 +73,108 @@ def tile_picked_lapl_none_e_kernel(
 
         minus_cols = keep.tile([P, PACK], F32, name="minus_cols")
         nc.scalar.mul(minus_cols[:], gate_cols[:], -1.0)
-        spread = psum.tile([P, PACK, P], F32, name="spread", tag="back0")
+        spread = psum.tile([P, PACK, P], F32, name="spread", tag="back1")
         for e in range(PACK):
             nc.tensor.transpose(spread[:, e, :], minus_cols[:, e : e + 1].to_broadcast([P, P]), ident[:])
+        minus_gate = keep.tile([P, 2, V], F32, name="minus_gate")
 
-        x_pick = keep.tile([P, S * PACK], BF16, name="x_pick", align_bytes=64)
-        picked = keep.tile([P, 2, S], U32, name="picked")
-        for u in range(2):
-            pairs = keep.tile([P, T * 2], BF16, name=f"x_pairs{u}", tag=f"x_pairs{u}", align_bytes=64)
-            for base, end, cut in X_LOADS[u]:
-                for lo, hi, copy in ((base, cut, nc.vector.tensor_copy), (cut, end, nc.scalar.copy)):
-                    if hi > lo:
-                        copy(
-                            pairs[:, 2 * lo : 2 * hi].rearrange("p (a i e) -> p a e i", i=4, e=2),
-                            x_raw[u, base][:, :, lo - base : hi - base].rearrange("p e (a i) -> p a e i", i=4),
-                        )
-            for lo, hi in GATHER_PARTS[u]:
-                nc.vector.tensor_copy(
-                    picked[:, u, lo:hi],
-                    pairs[:].bitcast(U32).indirect(offs_sb[:, lo // LIST : hi // LIST]),
-                )
+        def gather_on_vector(dst, window, places):
+            nc.vector.tensor_copy(dst, window.indirect(places))
 
-        w_cols = [raw[:].rearrange("p j (m t) -> p m j t", t=PACK) for raw in w_raw]
-        w_high = keep.tile([P, 2 * P * PACK], BF16, name="w_high", align_bytes=64)
-        high_dealt = w_high[:].rearrange("p (e q m j) -> p q m j e", e=2, q=4, j=PACK)
-        low_dealt = [keep.tile([P, P * PACK], BF16, name=f"w_low{c}", tag=f"w_low{c}", align_bytes=64) for c in range(2)]
+        def gather_on_scalar(dst, window, places):
+            nc.scalar.activation(dst, window.indirect(places), COPY)
 
-        def deal_low(q):
-            view = low_dealt[q // 2][:].rearrange("p (q m e j) -> p q m j e", q=2, e=2, j=PACK)
-            nc.scalar.copy(view[:, q % 2], w_cols[q][:, :, :, :2])
+        picked = [keep.tile([P, PACK, HALF_S], BF16, name=f"picked{half}") for half in range(2)]
 
-        def deal_high(q):
-            nc.scalar.copy(high_dealt[:, q], w_cols[q][:, :, :, 2:])
+        def pick(gather, j, lo, hi):
+            half, base = divmod(lo, HALF_S)
+            gather(picked[half][:, j, base : base + hi - lo], x_row[j][:], offs_sb[:, lo // LIST : hi // LIST])
 
-        deal_low(0)
-        deal_high(0)
-        for lo, hi in GATHER_PARTS[1]:
-            copy, word = (nc.vector.tensor_copy, I32) if lo else (nc.scalar.copy, U32)
-            copy(
-                x_pick[:].bitcast(word).rearrange("p (s u) -> p s u", u=2)[:, lo:hi, :],
-                picked[:, :, lo:hi].bitcast(word).rearrange("p u s -> p s u"),
+        x_dealt = [keep.tile([P, HALF_S * PACK], BF16, name=f"x_dealt{half}", align_bytes=64) for half in range(2)]
+
+        def place(half, u):
+            nc.vector.tensor_copy(
+                x_dealt[half][:].rearrange("p (c i j) -> p c j i", i=RUN, j=PACK)[:, :, 2 * u : 2 * u + 2, :],
+                picked[half][:, 2 * u : 2 * u + 2, :].rearrange("p j (c i) -> p c j i", i=RUN),
             )
 
-        def quantise(name, src, width, tag=None):
-            codes = keep.tile([P, width], U32, name=f"{name}_codes", tag=tag or f"{name}_codes", align_bytes=64)
-            plane = keep.tile([P, width], U8, name=f"{name}_plane", align_bytes=64)
-            nc.vector.quantize_mx(out=codes[:].bitcast(FP8X4), scales=plane[:], in_=src)
-            return codes, plane
-
-        x_codes, x_plane = {}, {}
-
-        def quantise_picked(base, end, tag):
-            codes = keep.tile([P, end - base], U32, name=f"x_codes{base}", tag=tag, align_bytes=64)
-            plane = keep.tile([P, end - base], U8, name=f"x_plane{base}", align_bytes=64)
-            for lo in range(0, end - base, PART):
-                x_codes[base + lo], x_plane[base + lo] = codes[:, lo:], plane[:, lo:]
-                first_col = PACK * (base + lo)
-                nc.vector.quantize_mx(
-                    out=codes[:, lo : lo + PART].bitcast(FP8X4),
-                    scales=plane[:, lo : lo + PART],
-                    in_=x_pick[:, first_col : first_col + PACK * PART],
+        for j in range(PACK):
+            cut = HALF_S if j < PACK - 1 else P
+            pick(gather_on_vector, j, 0, cut)
+            if cut < HALF_S:
+                pick(gather_on_scalar, j, cut, HALF_S)
+            pick(gather_on_scalar, j, HALF_S, S)
+            if j % 2:
+                place(0, j // 2)
+                place(1, j // 2)
+            if j == 0:
+                nc.scalar.copy(
+                    minus_gate[:].rearrange("p d (n e) -> p (d n) e", e=PACK), spread[:].rearrange("p e n -> p n e")
                 )
 
-        def project(acc, codes, plane, lo, hi):
-            for a, b in ((0, 128), (128, 384), (384, 512)) if hi - lo == S else ((lo, hi),):
-                nc.tensor.matmul_mx(
-                    out=acc[:, a - lo : b - lo],
-                    lhsT=codes.bitcast(FP8X4),
-                    lhsT_scale=plane,
-                    rhs=x_codes[a][:, : b - a].bitcast(FP8X4),
-                    rhs_scale=x_plane[a][:, : b - a],
-                    start=True,
-                    stop=True,
-                )
+        def quantise(codes, plane, src):
+            nc.vector.quantize_mx(out=codes.bitcast(FP8X4), scales=plane, in_=src)
+
+        w_codes = keep.tile([P, H], U32, name="w_codes", align_bytes=64)
+        w_plane = keep.tile([P, H], U8, name="w_plane", align_bytes=64)
+        x_plane = keep.tile([P, S], U8, name="x_plane", align_bytes=64)
+        x_codes = {}
+
+        def project(acc, n, lo, hi):
+            half, base = divmod(lo, HALF_S)
+            nc.tensor.matmul_mx(
+                out=acc,
+                lhsT=w_codes[:, n * P : (n + 1) * P].bitcast(FP8X4),
+                lhsT_scale=w_plane[:, n * P : (n + 1) * P],
+                rhs=x_codes[half][:, base : base + hi - lo].bitcast(FP8X4),
+                rhs_scale=x_plane[:, lo:hi],
+                start=True,
+                stop=True,
+            )
+
+        head_cols = w_head[:].rearrange("p q j (m t) -> p q m j t", t=PACK)
+        tail_cols = w_tail[:].rearrange("p j (m t) -> p m j t", t=PACK)
+        w_low = [
+            keep.tile([P, P * PACK], BF16, name=f"w_low{half}", tag=f"w_low{half}", align_bytes=64) for half in range(2)
+        ]
+        w_high = keep.tile([P, 2 * P * PACK], BF16, name="w_high", tag="w_high", align_bytes=64)
+
+        low_head = w_low[0][:].rearrange("p (q m e j) -> p q m j e", q=2, e=2, j=PACK)
+        for q in range(2):
+            nc.scalar.copy(low_head[:, q], head_cols[:, q, :, :, :2])
+        x_codes[0] = keep.tile([P, HALF_S], U32, name="x_codes0", align_bytes=64)
+        quantise(x_codes[0][:], x_plane[:, :HALF_S], x_dealt[0][:])
+        quantise(w_codes[:, :P], w_plane[:, :P], w_low[0][:])
+        x_codes[1] = keep.tile([P, HALF_S], U32, name="x_codes1", tag="w_low0", align_bytes=64)
+        for lo in range(0, HALF_S, P):
+            plane = x_plane[:, HALF_S + lo : HALF_S + lo + P]
+            quantise(x_codes[1][:, lo : lo + P], plane, x_dealt[1][:, PACK * lo : PACK * (lo + P)])
+        high_cols = w_high[:].rearrange("p (e q m j) -> p q m j e", e=2, q=4, j=PACK)
+        nc.scalar.copy(high_cols[:, :2], head_cols[:, :, :, :, 2:])
+        nc.vector.tensor_copy(w_low[1][:].rearrange("p (m e j) -> p m j e", e=2, j=PACK), tail_cols[:, :, :, :2])
+        nc.vector.tensor_copy(
+            w_high[:].rearrange("p (e h m j) -> p h m j e", e=2, h=2, j=PACK)[:, 1], tail_cols[:, :, :, 2:]
+        )
+
+        quantise(w_codes[:, P : 2 * P], w_plane[:, P : 2 * P], w_low[1][:])
 
         h_sb = [keep.tile([P, S], F32, name=f"h_sb{n}") for n in range(PACK)]
-        quantise_picked(0, PART, "x_codes0")
-        deal_low(1)
-        codes0, plane0 = quantise("w_low0", low_dealt[0][:], P, "x_pairs1")
-        deal_high(1)
-        quantise_picked(PART, S, "w_raw1")
-        late_parts = []
-        for tag, lo in zip(("bank_a", "bank_b", "bank_c", "back1"), range(0, S, PART)):
-            bank = psum.tile([P, PART], F32, name=f"h_part{lo}", tag=tag)
-            project(bank[:], codes0[:], plane0[:], lo, lo + PART)
-            if lo < S - PART:
-                nc.vector.tensor_copy(h_sb[0][:, lo : lo + PART], bank[:])
-            else:
-                late_parts.append((lo, bank))
+        for lo, hi, tag in ((0, HALF_S, "bank_a"), (HALF_S, S - P, "bank_b"), (S - P, S, "bank_d")):
+            bank = psum.tile([P, hi - lo], F32, name=f"h_part{lo}", tag=tag)
+            project(bank[:], 0, lo, hi)
+            nc.scalar.copy(h_sb[0][:, lo:hi], bank[:])
+        quantise(w_codes[:, 2 * P :], w_plane[:, 2 * P :], w_high[:])
 
-        for q in (2, 3):
-            deal_low(q)
-            deal_high(q)
-        codes1, plane1 = quantise("w_low1", low_dealt[1][:], P)
-        codes_high, plane_high = quantise("w_high", w_high[:], 2 * P)
-        for lo, bank in late_parts:
-            nc.scalar.copy(h_sb[0][:, lo : lo + PART], bank[:])
-        minus_gate = keep.tile([P, 2, V], F32, name="minus_gate", tag="w_raw3", align_bytes=64)
-        for d in range(2):
-            nc.scalar.copy(
-                minus_gate[:, d, :].rearrange("p (n e) -> p n e", e=PACK),
-                spread[:].rearrange("p e (d n) -> p d n e", d=2)[:, d],
-            )
-        bank_c = psum.tile([P, S], F32, name="bank_low1")
-        project(bank_c[:], codes1[:], plane1[:], 0, S)
-        nc.scalar.copy(h_sb[1][:], bank_c[:])
+        def make_h(n, tag):
+            bank = psum.tile([P, S], F32, name=f"h_bank{n}", tag=tag)
+            for lo in (0, HALF_S):
+                project(bank[:, lo : lo + HALF_S], n, lo, lo + HALF_S)
+            nc.scalar.copy(h_sb[n][:], bank[:])
 
+        def weighted(dst, n, places, d):
+            nc.vector.tensor_tensor(dst, h_sb[n][:].indirect(places[:]), minus_gate[:, d, :], MULT)
 
-        first = keep.tile([P, PACK, V], F32, name="first")
-        second = keep.tile([P, PACK, V], F32, name="second")
-        rest = keep.tile([P, PACK, V], F32, name="rest")
-
-        def fetch(dst, n, places, other, op, c=None):
-            cols = slice(0, V) if c is None else slice(c * HALF_V, (c + 1) * HALF_V)
-            window = h_sb[n][:].indirect(places[:, cols.start // LIST : cols.stop // LIST])
-            nc.vector.tensor_tensor(dst[:, n, cols], window, other[:, cols], op)
-
-        z = [keep.tile([P, HALF_V * PACK], BF16, name=f"z{c}", align_bytes=64) for c in range(2)]
-        turned = [psum.tile([P, 2, P], F32, name=f"turned{c}", tag=tag) for c, tag in enumerate(("bank_a", "bank_b"))]
-        back = [psum.tile([P, HALF_V], F32, name=f"back{c}", tag=f"back{c}") for c in range(2)]
+        turned = [psum.tile([P, 2, P], F32, name=f"turned{c}") for c in range(2)]
 
         def turn(term, n, begin, end):
             for c in range(2):
@@ -204,70 +182,83 @@ def tile_picked_lapl_none_e_kernel(
                 nc.tensor.matmul(turned[c][:, n, :], src, ident[:], start=begin, stop=end, is_transpose=True)
 
         for n in range(2):
-            centre = keep.tile([P, V], F32, name=f"centre{n}", tag=f"centre{n}", align_bytes=64)
-            nc.vector.tensor_copy(centre[:], h_sb[n][:].indirect(cen_sb[:]))
-            turn(centre, n, True, False)
-            fetch(first, n, pos1_sb, minus_gate[:, 0, :], MULT)
-            turn(first[:, n, :], n, False, False)
+            near = keep.tile([P, V], F32, name=f"near{n}")
+            weighted(near[:], n, pos1_sb, 0)
+            turn(near, n, True, False)
             if n == 0:
-                for e in range(2):
-                    bank = psum.tile([P, S], F32, name=f"bank_high{e}")
-                    project(bank[:], codes_high[:, e * P : (e + 1) * P], plane_high[:, e * P : (e + 1) * P], 0, S)
-                    nc.scalar.copy(h_sb[2 + e][:], bank[:])
-            fetch(second, n, pos2_sb, minus_gate[:, 1, :], MULT)
-            turn(second[:, n, :], n, False, True)
+                make_h(1, "bank_c")
+            own = keep.tile([P, V], F32, name=f"own{n}")
+            gather_on_scalar(own[:], h_sb[n][:], cen_sb[:])
+            turn(own, n, False, False)
+            far = keep.tile([P, V], F32, name=f"far{n}", tag=f"far{n}")
+            weighted(far[:], n, pos2_sb, 1)
+            make_h(2 + n, ("bank_a", "bank_d")[n])
+            turn(far, n, False, True)
+
+        first = keep.tile([P, 2, V], F32, name="first")
+        second = keep.tile([P, 2, V], F32, name="second")
+        centre = keep.tile([P, 2, V], F32, name="centre", tag="far1")
+        z = keep.tile([P, V * PACK], BF16, name="z", align_bytes=64)
+        back = [psum.tile([P, HALF_V], F32, name=f"back{c}", tag=f"back{c}") for c in range(2)]
+        halves = [slice(c * HALF_V, (c + 1) * HALF_V) for c in range(2)]
+
+        plain = keep.tile([P, V], F32, name="plain")
+        gather_on_scalar(plain[:], h_sb[2][:], pos2_sb[:])
+        for n in (2, 3):
+            weighted(first[:, n - 2, :], n, pos1_sb, 0)
+        nc.vector.tensor_tensor(second[:, 0, :], plain[:], minus_gate[:, 1, :], MULT)
+        for cols in halves:
+            window = h_sb[3][:].indirect(pos2_sb[:, cols.start // LIST : cols.stop // LIST])
+            nc.vector.tensor_tensor(second[:, 1, cols], window, minus_gate[:, 1, cols], MULT)
         for c in range(2):
             rows = keep.tile([P, 2 * P], BF16, name=f"z_rows{c}")
             nc.scalar.copy(rows[:], turned[c][:].rearrange("v g q -> v (g q)"))
             nc.tensor.transpose(back[c][:], rows[:].bitcast(F32), ident[:])
-            nc.scalar.copy(z[c][:].bitcast(F32).rearrange("p (v u) -> p v u", u=2)[:, :, 0], back[c][:])
+        for n in (2, 3):
+            gather_on_scalar(centre[:, n - 2, :], h_sb[n][:], cen_sb[:])
+        for c in range(2):
+            words = z[:, c * H : (c + 1) * H].bitcast(F32).rearrange("p (v u) -> p v u", u=2)
+            nc.scalar.copy(words[:, :, 0], back[c][:])
 
-        fetch(first, 2, pos1_sb, minus_gate[:, 0, :], MULT)
-        fetch(second, 2, pos2_sb, minus_gate[:, 1, :], MULT)
-        fetch(rest, 2, cen_sb, first[:, 2, :], ADD)
-
-        def finish(c):
-            cols = slice(c * HALF_V, (c + 1) * HALF_V)
+        rest = keep.tile([P, 2, V], F32, name="rest")
+        for cols in halves:
+            nc.vector.tensor_tensor(rest[:, :, cols], first[:, :, cols], second[:, :, cols], ADD)
+        for c, cols in enumerate(halves):
             nc.vector.tensor_tensor(
-                z[c][:].rearrange("p (a i t) -> p a t i", i=4, t=PACK)[:, :, 2:, :],
-                rest[:, 2:, cols].rearrange("p t (a i) -> p a t i", i=4),
-                second[:, 2:, cols].rearrange("p t (a i) -> p a t i", i=4),
+                z[:, c * H : (c + 1) * H].rearrange("p (a i t) -> p a t i", i=RUN, t=PACK)[:, :, 2:, :],
+                rest[:, :, cols].rearrange("p t (a i) -> p a t i", i=RUN),
+                centre[:, :, cols].rearrange("p t (a i) -> p a t i", i=RUN),
                 ADD,
             )
+        z_codes, z_plane = [], []
+        for c in range(2):
+            z_codes.append(keep.tile([P, HALF_V], U32, name=f"z_codes{c}", align_bytes=64))
+            z_plane.append(keep.tile([P, HALF_V], U8, name=f"z_plane{c}", align_bytes=64))
+            quantise(z_codes[c][:], z_plane[c][:], z[:, c * H : (c + 1) * H])
 
-        def second_product(acc, m, codes, plane):
+        def second_product(acc, m, c):
             nc.tensor.matmul_mx(
                 out=acc,
                 lhsT=w2_codes[:, 2 * m * P : 2 * (m + 1) * P].bitcast(FP4X4),
                 lhsT_scale=w2_plane[:, m * P : (m + 1) * P],
-                rhs=codes[:].bitcast(FP8X4),
-                rhs_scale=plane[:],
+                rhs=z_codes[c][:].bitcast(FP8X4),
+                rhs_scale=z_plane[c][:],
                 start=True,
                 stop=True,
             )
 
-        last = PACK - 1
-        fetch(first, last, pos1_sb, minus_gate[:, 0, :], MULT)
-        fetch(second, last, pos2_sb, minus_gate[:, 1, :], MULT)
-        fetch(rest, last, cen_sb, first[:, last, :], ADD, 0)
-        fetch(rest, last, cen_sb, first[:, last, :], ADD, 1)
-        finish(0)
-        finish(1)
-        z_codes0, z_plane0 = quantise("z0", z[0][:], HALF_V)
-        z_codes1, z_plane1 = quantise("z1", z[1][:], HALF_V)
-
         out_rows = out.rearrange("(m p) v -> p m v", p=P)
-        early_ps = psum.tile([P, 2, HALF_V], F32, name="early_ps", tag="bank_a")
+        early_ps = psum.tile([P, 2, HALF_V], F32, name="early_ps", tag="bank_b")
         for m in range(2):
-            second_product(early_ps[:, m, :], m, z_codes0, z_plane0)
+            second_product(early_ps[:, m, :], m, 0)
         early = keep.tile([P, 2, HALF_V], F32, name="early")
         nc.scalar.copy(early[:], early_ps[:])
         nc.sync.dma_start(out_rows[:, :, :HALF_V], early[:])
         for m, (tag, copy, queue) in enumerate(
-            (("bank_b", nc.scalar.copy, nc.scalar), ("bank_c", nc.vector.tensor_copy, nc.sync))
+            (("bank_c", nc.scalar.copy, nc.scalar), ("bank_d", nc.vector.tensor_copy, nc.sync))
         ):
             late_ps = psum.tile([P, HALF_V], F32, name=f"late_ps{m}", tag=tag)
-            second_product(late_ps[:], m, z_codes1, z_plane1)
+            second_product(late_ps[:], m, 1)
             late = keep.tile([P, HALF_V], F32, name=f"late{m}")
             copy(late[:], late_ps[:])
             queue.dma_start(out_rows[:, m, HALF_V:], late[:])

@@ -174,12 +174,13 @@ def tile_picked_lapl_none_e_kernel(
         def weighted(dst, n, places, d):
             nc.vector.tensor_tensor(dst, h_sb[n][:].indirect(places[:]), minus_gate[:, d, :], MULT)
 
-        turned = [psum.tile([P, 2, P], F32, name=f"turned{c}") for c in range(2)]
+        turned = psum.tile([P, 2, 2, P], F32, name="turned")
 
         def turn(term, n, begin, end):
             for c in range(2):
                 src = term[:, c * HALF_V : (c + 1) * HALF_V]
-                nc.tensor.matmul(turned[c][:, n, :], src, ident[:], start=begin, stop=end, is_transpose=True)
+                first_pass, last_pass = begin and n == 0 and c == 0, end and n == 1 and c == 1
+                nc.tensor.matmul(turned[:, c, n, :], src, ident[:], start=first_pass, stop=last_pass, is_transpose=True)
 
         for n in range(2):
             near = keep.tile([P, V], F32, name=f"near{n}")
@@ -199,7 +200,7 @@ def tile_picked_lapl_none_e_kernel(
         second = keep.tile([P, 2, V], F32, name="second")
         centre = keep.tile([P, 2, V], F32, name="centre", tag="far1")
         z = keep.tile([P, V * PACK], BF16, name="z", align_bytes=64)
-        back = [psum.tile([P, HALF_V], F32, name=f"back{c}", tag=f"back{c}") for c in range(2)]
+        back = psum.tile([P, V], F32, name="back", tag="back1")
         halves = [slice(c * HALF_V, (c + 1) * HALF_V) for c in range(2)]
 
         plain = keep.tile([P, V], F32, name="plain")
@@ -210,15 +211,13 @@ def tile_picked_lapl_none_e_kernel(
         for cols in halves:
             window = h_sb[3][:].indirect(pos2_sb[:, cols.start // LIST : cols.stop // LIST])
             nc.vector.tensor_tensor(second[:, 1, cols], window, minus_gate[:, 1, cols], MULT)
-        for c in range(2):
-            rows = keep.tile([P, 2 * P], BF16, name=f"z_rows{c}")
-            nc.scalar.copy(rows[:], turned[c][:].rearrange("v g q -> v (g q)"))
-            nc.tensor.transpose(back[c][:], rows[:].bitcast(F32), ident[:])
+        rows = keep.tile([P, H], BF16, name="rows")
+        nc.scalar.copy(rows[:], turned[:].rearrange("v c g q -> v (c g q)"))
+        for cols in halves:
+            nc.tensor.transpose(back[:, cols], rows[:].bitcast(F32)[:, cols], ident[:])
         for n in (2, 3):
             gather_on_scalar(centre[:, n - 2, :], h_sb[n][:], cen_sb[:])
-        for c in range(2):
-            words = z[:, c * H : (c + 1) * H].bitcast(F32).rearrange("p (v u) -> p v u", u=2)
-            nc.scalar.copy(words[:, :, 0], back[c][:])
+        nc.scalar.copy(z[:].bitcast(F32).rearrange("p (v u) -> p v u", u=2)[:, :, 0], back[:])
 
         rest = keep.tile([P, 2, V], F32, name="rest")
         for cols in halves:

@@ -92,10 +92,10 @@ def tile_picked_lapl_none_e_kernel(
 
         x_dealt = [keep.tile([P, HALF_S * PACK], BF16, name=f"x_dealt{half}", align_bytes=64) for half in range(2)]
 
-        def place(half, u):
+        def place(half):
             nc.vector.tensor_copy(
-                x_dealt[half][:].rearrange("p (c i j) -> p c j i", i=RUN, j=PACK)[:, :, 2 * u : 2 * u + 2, :],
-                picked[half][:, 2 * u : 2 * u + 2, :].rearrange("p j (c i) -> p c j i", i=RUN),
+                x_dealt[half][:].rearrange("p (c i j) -> p c j i", i=RUN, j=PACK),
+                picked[half][:].rearrange("p j (c i) -> p c j i", i=RUN),
             )
 
         for j in range(PACK):
@@ -104,13 +104,13 @@ def tile_picked_lapl_none_e_kernel(
             if cut < HALF_S:
                 pick(gather_on_scalar, j, cut, HALF_S)
             pick(gather_on_scalar, j, HALF_S, S)
-            if j % 2:
-                place(0, j // 2)
-                place(1, j // 2)
             if j == 0:
                 nc.scalar.copy(
                     minus_gate[:].rearrange("p d (n e) -> p (d n) e", e=PACK), spread[:].rearrange("p e n -> p n e")
                 )
+
+        place(0)
+        place(1)
 
         def quantise(codes, plane, src):
             nc.vector.quantize_mx(out=codes.bitcast(FP8X4), scales=plane, in_=src)

@@ -165,11 +165,13 @@ def tile_picked_lapl_none_e_kernel(
             nc.scalar.copy(h_sb[0][:, lo:hi], bank[:])
         quantise(w_codes[:, 2 * P :], w_plane[:, 2 * P :], w_high[:])
 
-        def make_h(n, tag):
-            bank = psum.tile([P, S], F32, name=f"h_bank{n}", tag=tag)
-            for lo in (0, HALF_S):
-                project(bank[:, lo : lo + HALF_S], n, lo, lo + HALF_S)
-            nc.scalar.copy(h_sb[n][:], bank[:])
+        def make_h(n, tags):
+            width = S // len(tags)
+            for base, tag in zip(range(0, S, width), tags):
+                bank = psum.tile([P, width], F32, name=f"h_bank{n}_{base}", tag=tag)
+                for lo in range(0, width, HALF_S):
+                    project(bank[:, lo : lo + HALF_S], n, base + lo, base + lo + HALF_S)
+                nc.scalar.copy(h_sb[n][:, base : base + width], bank[:])
 
         def weighted(dst, n, places, d):
             nc.vector.tensor_tensor(dst, h_sb[n][:].indirect(places[:]), minus_gate[:, d, :], MULT)
@@ -187,13 +189,13 @@ def tile_picked_lapl_none_e_kernel(
             weighted(near[:], n, pos1_sb, 0)
             turn(near, n, True, False)
             if n == 0:
-                make_h(1, "bank_c")
+                make_h(1, ("bank_c", "bank_e"))
             own = keep.tile([P, V], F32, name=f"own{n}")
             gather_on_scalar(own[:], h_sb[n][:], cen_sb[:])
             turn(own, n, False, False)
             far = keep.tile([P, V], F32, name=f"far{n}", tag=f"far{n}")
             weighted(far[:], n, pos2_sb, 1)
-            make_h(2 + n, ("bank_a", "bank_d")[n])
+            make_h(2 + n, (("bank_f", "bank_a"), ("bank_d",))[n])
             turn(far, n, False, True)
 
         first = keep.tile([P, 2, V], F32, name="first")

@@ -256,7 +256,7 @@ def tile_picked_lapl_none_e_kernel(
         nc.scalar.copy(early[:], early_ps[:])
         nc.sync.dma_start(out_rows[:, :, :HALF_V], early[:])
         for m, (tag, copy, queue) in enumerate(
-            (("bank_c", nc.scalar.copy, nc.scalar), ("bank_d", nc.vector.tensor_copy, nc.sync))
+            (("bank_c", nc.vector.tensor_copy, nc.sync), ("bank_d", nc.scalar.copy, nc.scalar))
         ):
             late_ps = psum.tile([P, HALF_V], F32, name=f"late_ps{m}", tag=tag)
             second_product(late_ps[:], m, 1)

@@ -25,6 +25,7 @@ HALF_S = S // 2
 HALF_H = H // 2
 HALF_V = V // 2
 RUN = 4
+EARLY_SHARE = 64
 
 
 def tile_picked_lapl_none_e_kernel(
@@ -84,33 +85,35 @@ def tile_picked_lapl_none_e_kernel(
         def gather_on_scalar(dst, window, places):
             nc.scalar.activation(dst, window.indirect(places), COPY)
 
-        picked = [keep.tile([P, PACK, HALF_S], BF16, name=f"picked{half}") for half in range(2)]
-
-        def pick(gather, j, lo, hi):
-            half, base = divmod(lo, HALF_S)
-            gather(picked[half][:, j, base : base + hi - lo], x_row[j][:], offs_sb[:, lo // LIST : hi // LIST])
-
         x_dealt = [keep.tile([P, HALF_S * PACK], BF16, name=f"x_dealt{half}", align_bytes=64) for half in range(2)]
+        picked = keep.tile([P, PACK, S - P], BF16, name="picked")
 
-        def place(half):
+        def place(lo):
+            half, base = divmod(lo, HALF_S)
             nc.vector.tensor_copy(
-                x_dealt[half][:].rearrange("p (c i j) -> p c j i", i=RUN, j=PACK),
-                picked[half][:].rearrange("p j (c i) -> p c j i", i=RUN),
+                x_dealt[half][:, PACK * base : PACK * (base + P)].rearrange("p (c i j) -> p c j i", i=RUN, j=PACK),
+                picked[:, :, lo - P : lo].rearrange("p j (c i) -> p c j i", i=RUN),
             )
 
+        def pick(gather, j, lo, hi):
+            gather(picked[:, j, lo - P : hi - P], x_row[j][:], offs_sb[:, lo // LIST : hi // LIST])
+
+        direct = x_dealt[0][:, : PACK * P].rearrange("p (c j) -> p c j", j=PACK)
         for j in range(PACK):
-            cut = HALF_S if j < PACK - 1 else P
-            pick(gather_on_vector, j, 0, cut)
-            if cut < HALF_S:
-                pick(gather_on_scalar, j, cut, HALF_S)
-            pick(gather_on_scalar, j, HALF_S, S)
+            gather_on_vector(direct[:, :, j], x_row[j][:], offs_sb[:, : P // LIST])
+            if j < PACK - 1:
+                pick(gather_on_vector, j, P, P + EARLY_SHARE)
+                pick(gather_on_scalar, j, P + EARLY_SHARE, S)
+            else:
+                for lo in range(P, S, P):
+                    pick(gather_on_scalar, j, lo, lo + P)
             if j == 0:
                 nc.scalar.copy(
                     minus_gate[:].rearrange("p d (n e) -> p (d n) e", e=PACK), spread[:].rearrange("p e n -> p n e")
                 )
 
-        place(0)
-        place(1)
+        place(P)
+        place(2 * P)
 
         def quantise(codes, plane, src):
             nc.vector.quantize_mx(out=codes.bitcast(FP8X4), scales=plane, in_=src)
@@ -144,6 +147,7 @@ def tile_picked_lapl_none_e_kernel(
             nc.scalar.copy(low_head[:, q], head_cols[:, q, :, :, :2])
         x_codes[0] = keep.tile([P, HALF_S], U32, name="x_codes0", align_bytes=64)
         quantise(x_codes[0][:], x_plane[:, :HALF_S], x_dealt[0][:])
+        place(3 * P)
         quantise(w_codes[:, :P], w_plane[:, :P], w_low[0][:])
         x_codes[1] = keep.tile([P, HALF_S], U32, name="x_codes1", tag="w_low0", align_bytes=64)
         for lo in range(0, HALF_S, P):

@@ -25,7 +25,6 @@ HALF_S = S // 2
 HALF_H = H // 2
 HALF_V = V // 2
 RUN = 4
-EARLY_SHARE = 64
 
 
 def tile_picked_lapl_none_e_kernel(
@@ -86,34 +85,36 @@ def tile_picked_lapl_none_e_kernel(
             nc.scalar.activation(dst, window.indirect(places), COPY)
 
         x_dealt = [keep.tile([P, HALF_S * PACK], BF16, name=f"x_dealt{half}", align_bytes=64) for half in range(2)]
-        picked = keep.tile([P, PACK, S - P], BF16, name="picked")
+        picked = keep.tile([P, PACK, S], BF16, name="picked")
 
-        def place(lo):
+        def place(lo, rows):
             half, base = divmod(lo, HALF_S)
+            dealt = x_dealt[half][:, PACK * base : PACK * (base + P)].rearrange("p (c i j) -> p c j i", i=RUN, j=PACK)
             nc.vector.tensor_copy(
-                x_dealt[half][:, PACK * base : PACK * (base + P)].rearrange("p (c i j) -> p c j i", i=RUN, j=PACK),
-                picked[:, :, lo - P : lo].rearrange("p j (c i) -> p c j i", i=RUN),
+                dealt[:, :, :rows, :], picked[:, :rows, lo : lo + P].rearrange("p j (c i) -> p c j i", i=RUN)
             )
 
         def pick(gather, j, lo, hi):
-            gather(picked[:, j, lo - P : hi - P], x_row[j][:], offs_sb[:, lo // LIST : hi // LIST])
+            gather(picked[:, j, lo:hi], x_row[j][:], offs_sb[:, lo // LIST : hi // LIST])
 
-        direct = x_dealt[0][:, : PACK * P].rearrange("p (c j) -> p c j", j=PACK)
-        for j in range(PACK):
-            gather_on_vector(direct[:, :, j], x_row[j][:], offs_sb[:, : P // LIST])
-            if j < PACK - 1:
-                pick(gather_on_vector, j, P, P + EARLY_SHARE)
-                pick(gather_on_scalar, j, P + EARLY_SHARE, S)
-            else:
-                for lo in range(P, S, P):
-                    pick(gather_on_scalar, j, lo, lo + P)
+        last = PACK - 1
+        for j in range(last):
+            width = HALF_S if j < last - 1 else P
+            for lo in range(0, HALF_S, width):
+                pick(gather_on_vector, j, lo, lo + width)
+            pick(gather_on_scalar, j, HALF_S, S)
             if j == 0:
                 nc.scalar.copy(
                     minus_gate[:].rearrange("p d (n e) -> p (d n) e", e=PACK), spread[:].rearrange("p e n -> p n e")
                 )
+        place(0, last)
+        direct = x_dealt[0][:, : PACK * P].rearrange("p (c j) -> p c j", j=PACK)
+        gather_on_vector(direct[:, :, last], x_row[last][:], offs_sb[:, : P // LIST])
+        for lo in range(P, S, P):
+            pick(gather_on_scalar, last, lo, lo + P)
 
-        place(P)
-        place(2 * P)
+        place(P, PACK)
+        place(2 * P, PACK)
 
         def quantise(codes, plane, src):
             nc.vector.quantize_mx(out=codes.bitcast(FP8X4), scales=plane, in_=src)
@@ -147,7 +148,7 @@ def tile_picked_lapl_none_e_kernel(
             nc.scalar.copy(low_head[:, q], head_cols[:, q, :, :, :2])
         x_codes[0] = keep.tile([P, HALF_S], U32, name="x_codes0", align_bytes=64)
         quantise(x_codes[0][:], x_plane[:, :HALF_S], x_dealt[0][:])
-        place(3 * P)
+        place(3 * P, PACK)
         quantise(w_codes[:, :P], w_plane[:, :P], w_low[0][:])
         x_codes[1] = keep.tile([P, HALF_S], U32, name="x_codes1", tag="w_low0", align_bytes=64)
         for lo in range(0, HALF_S, P):

from contextlib import ExitStack

import concourse.mybir as mybir
from concourse.masks import make_identity

K, T, S, V, H, N = 512, 1024, 512, 256, 512, 256
FLOPS = 2 * K * H * S + 2 * H * N * V

F32 = mybir.dt.float32
BF16 = mybir.dt.bfloat16
I32 = mybir.dt.int32
U32 = mybir.dt.uint32
U16 = mybir.dt.uint16
U8 = mybir.dt.uint8
FP8X4 = mybir.dt.float8_e4m3fn_x4
FP4X4 = mybir.dt.float4_e2m1fn_x4
MULT = mybir.AluOpType.mult
ADD = mybir.AluOpType.add
COPY = mybir.ActivationFunctionType.Copy

P = 128
PACK = 4
LIST = 16
HALF_S = S // 2
HALF_H = H // 2
HALF_V = V // 2
RUN = 4


def tile_picked_lapl_none_e_kernel(
    tc, xT, w1, w2_words, w2_scales, gate, offs, cen, pos1, pos2, out
):
    nc = tc.nc
    with ExitStack() as ctx:
        keep = ctx.enter_context(tc.tile_pool(name="keep", bufs=1))
        psum = ctx.enter_context(tc.psum_pool(name="psum", bufs=1))

        offs_sb = keep.tile([P, S // LIST], U16, name="offs_sb")
        cen_sb = keep.tile([P, V // LIST], U16, name="cen_sb")
        pos1_sb = keep.tile([P, V // LIST], U16, name="pos1_sb")
        pos2_sb = keep.tile([P, V // LIST], U16, name="pos2_sb")
        both_rows = gate.rearrange("d p v -> (d p v)")[(P - 1) * V : (P + 1) * V]
        gate_cols = keep.tile([P, PACK], F32, name="gate_cols")
        nc.scalar.dma_start(gate_cols[:], both_rows.rearrange("(p e) -> p e", e=PACK))
        w2_codes = keep.tile([P, 2 * N], U8, name="w2_codes", align_bytes=64)
        w2_plane = keep.tile([P, N], U8, name="w2_plane", align_bytes=64)
        nc.gpsimd.memset(w2_plane[:], 0)
        ident = keep.tile([P, P], F32, name="ident")
        make_identity(nc, ident[:])

        x_rows = xT.rearrange("(p j) t -> p j t", j=PACK)
        w_rows = w1.rearrange("(p j) c -> p j c", j=PACK)
        x_row = []
        for j in range(PACK):
            row = keep.tile([P, T], F32, name=f"x_row{j}")
            nc.sync.dma_start(row[:], x_rows[:, j, :])
            x_row.append(row)
            if j == 0:
                nc.sync.dma_start(offs_sb[:], offs)
        w_head = keep.tile([P, 2, PACK, P], F32, name="w_head")
        for q in range(2):
            nc.sync.dma_start(w_head[:, q], w_rows[:, :, q * P : (q + 1) * P])
        w_tail = keep.tile([P, PACK, HALF_H], F32, name="w_tail")
        nc.sync.dma_start(w_tail[:], w_rows[:, :, HALF_H:])
        nc.sync.dma_start(cen_sb[:], cen)
        nc.sync.dma_start(pos1_sb[:], pos1)
        nc.sync.dma_start(pos2_sb[:], pos2)
        nc.sync.dma_start(w2_codes[:].bitcast(I32), w2_words[0].bitcast(I32))
        for q in range(4):
            nc.sync.dma_start(
                w2_plane[32 * q : 32 * q + 4, :].bitcast(I32), w2_scales[0, 4 * q : 4 * q + 4, :].bitcast(I32)
            )

        minus_cols = keep.tile([P, PACK], F32, name="minus_cols")
        nc.scalar.mul(minus_cols[:], gate_cols[:], -1.0)
        spread = psum.tile([P, PACK, P], F32, name="spread", tag="back1")
        for e in range(PACK):
            nc.tensor.transpose(spread[:, e, :], minus_cols[:, e : e + 1].to_broadcast([P, P]), ident[:])
        minus_gate = keep.tile([P, 2, V], F32, name="minus_gate")

        def gather_on_vector(dst, window, places):
            nc.vector.tensor_copy(dst, window.indirect(places))

        def gather_on_scalar(dst, window, places):
            nc.scalar.activation(dst, window.indirect(places), COPY)

        x_dealt = [keep.tile([P, HALF_S * PACK], BF16, name=f"x_dealt{half}", align_bytes=64) for half in range(2)]
        picked = keep.tile([P, PACK, S], BF16, name="picked")

        def place(lo, rows):
            half, base = divmod(lo, HALF_S)
            dealt = x_dealt[half][:, PACK * base : PACK * (base + P)].rearrange("p (c i j) -> p c j i", i=RUN, j=PACK)
            nc.vector.tensor_copy(
                dealt[:, :, :rows, :], picked[:, :rows, lo : lo + P].rearrange("p j (c i) -> p c j i", i=RUN)
            )

        def pick(gather, j, lo, hi):
            gather(picked[:, j, lo:hi], x_row[j][:], offs_sb[:, lo // LIST : hi // LIST])

        last = PACK - 1
        for j in range(last):
            width = HALF_S if j < last - 1 else P
            for lo in range(0, HALF_S, width):
                pick(gather_on_vector, j, lo, lo + width)
            pick(gather_on_scalar, j, HALF_S, S)
            if j == 0:
                nc.scalar.copy(
                    minus_gate[:].rearrange("p d (n e) -> p (d n) e", e=PACK), spread[:].rearrange("p e n -> p n e")
                )
        place(0, last)
        direct = x_dealt[0][:, : PACK * P].rearrange("p (c j) -> p c j", j=PACK)
        gather_on_vector(direct[:, :, last], x_row[last][:], offs_sb[:, : P // LIST])
        for lo in range(P, S, P):
            pick(gather_on_scalar, last, lo, lo + P)

        place(P, PACK)
        place(2 * P, PACK)

        def quantise(codes, plane, src):
            nc.vector.quantize_mx(out=codes.bitcast(FP8X4), scales=plane, in_=src)

        w_codes = keep.tile([P, H], U32, name="w_codes", align_bytes=64)
        w_plane = keep.tile([P, H], U8, name="w_plane", align_bytes=64)
        x_plane = keep.tile([P, S], U8, name="x_plane", align_bytes=64)
        x_codes = {}

        def project(acc, n, lo, hi):
            half, base = divmod(lo, HALF_S)
            nc.tensor.matmul_mx(
                out=acc,
                lhsT=w_codes[:, n * P : (n + 1) * P].bitcast(FP8X4),
                lhsT_scale=w_plane[:, n * P : (n + 1) * P],
                rhs=x_codes[half][:, base : base + hi - lo].bitcast(FP8X4),
                rhs_scale=x_plane[:, lo:hi],
                start=True,
                stop=True,
            )

        head_cols = w_head[:].rearrange("p q j (m t) -> p q m j t", t=PACK)
        tail_cols = w_tail[:].rearrange("p j (m t) -> p m j t", t=PACK)
        w_low = [
            keep.tile([P, P * PACK], BF16, name=f"w_low{half}", tag=f"w_low{half}", align_bytes=64) for half in range(2)
        ]
        w_high = keep.tile([P, 2 * P * PACK], BF16, name="w_high", tag="w_high", align_bytes=64)

        low_head = w_low[0][:].rearrange("p (q m e j) -> p q m j e", q=2, e=2, j=PACK)
        for q in range(2):
            nc.scalar.copy(low_head[:, q], head_cols[:, q, :, :, :2])
        x_codes[0] = keep.tile([P, HALF_S], U32, name="x_codes0", align_bytes=64)
        quantise(x_codes[0][:], x_plane[:, :HALF_S], x_dealt[0][:])
        place(3 * P, PACK)
        quantise(w_codes[:, :P], w_plane[:, :P], w_low[0][:])
        x_codes[1] = keep.tile([P, HALF_S], U32, name="x_codes1", tag="w_low0", align_bytes=64)
        for lo in range(0, HALF_S, P):
            plane = x_plane[:, HALF_S + lo : HALF_S + lo + P]
            quantise(x_codes[1][:, lo : lo + P], plane, x_dealt[1][:, PACK * lo : PACK * (lo + P)])
        high_cols = w_high[:].rearrange("p (e q m j) -> p q m j e", e=2, q=4, j=PACK)
        nc.scalar.copy(high_cols[:, :2], head_cols[:, :, :, :, 2:])
        nc.vector.tensor_copy(w_low[1][:].rearrange("p (m e j) -> p m j e", e=2, j=PACK), tail_cols[:, :, :, :2])
        nc.vector.tensor_copy(
            w_high[:].rearrange("p (e h m j) -> p h m j e", e=2, h=2, j=PACK)[:, 1], tail_cols[:, :, :, 2:]
        )

        quantise(w_codes[:, P : 2 * P], w_plane[:, P : 2 * P], w_low[1][:])

        h_sb = [keep.tile([P, S], F32, name=f"h_sb{n}") for n in range(PACK)]
        for lo, hi, tag in ((0, HALF_S, "bank_a"), (HALF_S, S - P, "bank_b"), (S - P, S, "bank_d")):
            bank = psum.tile([P, hi - lo], F32, name=f"h_part{lo}", tag=tag)
            project(bank[:], 0, lo, hi)
            nc.scalar.copy(h_sb[0][:, lo:hi], bank[:])
        quantise(w_codes[:, 2 * P :], w_plane[:, 2 * P :], w_high[:])

        def make_h(n, tags):
            width = S // len(tags)
            for base, tag in zip(range(0, S, width), tags):
                bank = psum.tile([P, width], F32, name=f"h_bank{n}_{base}", tag=tag)
                for lo in range(0, width, HALF_S):
                    project(bank[:, lo : lo + HALF_S], n, base + lo, base + lo + HALF_S)
                nc.scalar.copy(h_sb[n][:, base : base + width], bank[:])

        def weighted(dst, n, places, d):
            nc.vector.tensor_tensor(dst, h_sb[n][:].indirect(places[:]), minus_gate[:, d, :], MULT)

        turned = psum.tile([P, 2, 2, P], F32, name="turned")

        def turn(term, n, begin, end):
            for c in range(2):
                src = term[:, c * HALF_V : (c + 1) * HALF_V]
                first_pass, last_pass = begin and n == 0 and c == 0, end and n == 1 and c == 1
                nc.tensor.matmul(turned[:, c, n, :], src, ident[:], start=first_pass, stop=last_pass, is_transpose=True)

        for n in range(2):
            near = keep.tile([P, V], F32, name=f"near{n}")
            weighted(near[:], n, pos1_sb, 0)
            turn(near, n, True, False)
            if n == 0:
                make_h(1, ("bank_c", "bank_e"))
            own = keep.tile([P, V], F32, name=f"own{n}")
            gather_on_scalar(own[:], h_sb[n][:], cen_sb[:])
            turn(own, n, False, False)
            far = keep.tile([P, V], F32, name=f"far{n}", tag=f"far{n}")
            weighted(far[:], n, pos2_sb, 1)
            make_h(2 + n, (("bank_f", "bank_a"), ("bank_d",))[n])
            turn(far, n, False, True)

        first = keep.tile([P, 2, V], F32, name="first")
        second = keep.tile([P, 2, V], F32, name="second")
        centre = keep.tile([P, 2, V], F32, name="centre", tag="far1")
        z = keep.tile([P, V * PACK], BF16, name="z", align_bytes=64)
        back = psum.tile([P, V], F32, name="back", tag="back1")
        halves = [slice(c * HALF_V, (c + 1) * HALF_V) for c in range(2)]

        plain = keep.tile([P, V], F32, name="plain")
        gather_on_scalar(plain[:], h_sb[2][:], pos2_sb[:])
        for n in (2, 3):
            weighted(first[:, n - 2, :], n, pos1_sb, 0)
        nc.vector.tensor_tensor(second[:, 0, :], plain[:], minus_gate[:, 1, :], MULT)
        for cols in halves:
            window = h_sb[3][:].indirect(pos2_sb[:, cols.start // LIST : cols.stop // LIST])
            nc.vector.tensor_tensor(second[:, 1, cols], window, minus_gate[:, 1, cols], MULT)
        rows = keep.tile([P, H], BF16, name="rows")
        nc.scalar.copy(rows[:], turned[:].rearrange("v c g q -> v (c g q)"))
        for cols in halves:
            nc.tensor.transpose(back[:, cols], rows[:].bitcast(F32)[:, cols], ident[:])
        for n in (2, 3):
            gather_on_scalar(centre[:, n - 2, :], h_sb[n][:], cen_sb[:])
        nc.scalar.copy(z[:].bitcast(F32).rearrange("p (v u) -> p v u", u=2)[:, :, 0], back[:])

        rest = keep.tile([P, 2, V], F32, name="rest")
        for cols in halves:
            nc.vector.tensor_tensor(rest[:, :, cols], first[:, :, cols], second[:, :, cols], ADD)
        for c, cols in enumerate(halves):
            nc.vector.tensor_tensor(
                z[:, c * H : (c + 1) * H].rearrange("p (a i t) -> p a t i", i=RUN, t=PACK)[:, :, 2:, :],
                rest[:, :, cols].rearrange("p t (a i) -> p a t i", i=RUN),
                centre[:, :, cols].rearrange("p t (a i) -> p a t i", i=RUN),
                ADD,
            )
        z_codes, z_plane = [], []
        for c in range(2):
            z_codes.append(keep.tile([P, HALF_V], U32, name=f"z_codes{c}", align_bytes=64))
            z_plane.append(keep.tile([P, HALF_V], U8, name=f"z_plane{c}", align_bytes=64))
            quantise(z_codes[c][:], z_plane[c][:], z[:, c * H : (c + 1) * H])

        def second_product(acc, m, c):
            nc.tensor.matmul_mx(
                out=acc,
                lhsT=w2_codes[:, 2 * m * P : 2 * (m + 1) * P].bitcast(FP4X4),
                lhsT_scale=w2_plane[:, m * P : (m + 1) * P],
                rhs=z_codes[c][:].bitcast(FP8X4),
                rhs_scale=z_plane[c][:],
                start=True,
                stop=True,
            )

        out_rows = out.rearrange("(m p) v -> p m v", p=P)
        early_ps = psum.tile([P, 2, HALF_V], F32, name="early_ps", tag="bank_b")
        for m in range(2):
            second_product(early_ps[:, m, :], m, 0)
        early = keep.tile([P, 2, HALF_V], F32, name="early")
        nc.scalar.copy(early[:], early_ps[:])
        nc.sync.dma_start(out_rows[:, :, :HALF_V], early[:])
        for m, (tag, copy, queue) in enumerate(
            (("bank_c", nc.vector.tensor_copy, nc.sync), ("bank_d", nc.scalar.copy, nc.scalar))
        ):
            late_ps = psum.tile([P, HALF_V], F32, name=f"late_ps{m}", tag=tag)
            second_product(late_ps[:], m, 1)
            late = keep.tile([P, HALF_V], F32, name=f"late{m}")
            copy(late[:], late_ps[:])
            queue.dma_start(out_rows[:, m, HALF_V:], late[:])
